import numpy as np
import ml_dtypes


def mxq(x, axis, fmt="e4m3"):
    dtype, down = {"e4m3": (ml_dtypes.float8_e4m3fn, 7), "e5m2": (ml_dtypes.float8_e5m2, 14)}[fmt]
    v = np.moveaxis(np.asarray(x, np.float32).astype(ml_dtypes.bfloat16).astype(np.float64), axis, -1)
    blocks = v.reshape(v.shape[:-1] + (-1, 32))
    amax = np.abs(blocks).max(-1, keepdims=True)
    byte = np.maximum(np.where(amax > 0, np.frexp(amax)[1] - 1 + 127, 0) - down, 1)
    scale = np.exp2(byte - 127.0)
    codes = (blocks / scale).astype(np.float32).astype(dtype).astype(np.float64)
    return np.moveaxis((codes * scale).reshape(v.shape), -1, axis)


WIDE = False


def mx_kscale(k):
    if not WIDE:
        return np.ones(k)
    levels = np.array([10, -10, 5, -5, 0])
    if k % 512:
        return np.exp2(np.random.permutation(np.resize(levels, k // 32))).repeat(32)
    a = np.empty((k // 512, 16))
    for p in range(k // 512):
        a[p, :8] = np.random.permutation(np.resize(levels, 8))
        for g in range(8):
            far = levels[np.abs(levels - a[p, g]) >= 10]
            a[p, g + 8] = far[np.random.randint(len(far))]
    return np.exp2(a.ravel()).repeat(32)


def f64(x):
    return np.asarray(x).astype(np.float64)


def striped(idx):
    return np.tile(idx.reshape(-1, 16).T, (8, 1)).astype(np.uint16)


def unstriped(offs):
    return offs[:16].T.reshape(-1).astype(np.int64)


E2M1 = np.array([0.0, 0.5, 1.0, 1.5, 2.0, 3.0, 4.0, 6.0, -0.0, -0.5, -1.0, -1.5, -2.0, -3.0, -4.0, -6.0])


def pack_weight(w, fmt):
    k, n = w.shape
    w = f64(np.asarray(w, np.float32).astype(ml_dtypes.bfloat16)).reshape(k // 32, 32, n)
    amax = np.abs(w).max(1)
    if fmt == "e4m3":
        byte = np.frexp(amax)[1] - 1 + 127 - 7
    else:
        mant, ex = np.frexp(amax / 6.0)
        byte = np.where(mant > 0.5, ex, ex - 1) + 127
    byte = np.clip(np.where(amax > 0, byte, 1), 1, 254)
    scaled = (w * np.exp2(127.0 - byte)[:, None, :]).reshape(k, n).astype(np.float32)
    by_word = np.ascontiguousarray(scaled.reshape(k // 512, 128, 4, n).transpose(0, 1, 3, 2))
    if fmt == "e4m3":
        words = by_word.astype(ml_dtypes.float8_e4m3fn).view(np.uint8)
    else:
        c = by_word.astype(ml_dtypes.float4_e2m1fn).view(np.uint8) & 0xF
        words = (c[..., 0::2] | (c[..., 1::2] << 4)).reshape(k // 512, 128, 2 * n)
    return np.ascontiguousarray(words), np.ascontiguousarray(byte.astype(np.uint8).reshape(k // 512, 16, n))


def unpack_weight(words, scales, fmt):
    g, _, n = scales.shape
    words = np.ascontiguousarray(words).reshape(g, 128, n, -1)
    if fmt == "e4m3":
        vals = words.view(ml_dtypes.float8_e4m3fn).astype(np.float64)
    else:
        nib = np.empty((g, 128, n, 4), np.uint8)
        nib[..., 0::2] = words & 0xF
        nib[..., 1::2] = words >> 4
        vals = E2M1[nib]
    vals = vals * np.repeat(np.exp2(scales.astype(np.float64) - 127.0), 8, axis=1)[..., None]
    return vals.transpose(0, 1, 3, 2).reshape(g * 512, n)


def silu(v):
    return v / (1.0 + np.exp(-np.maximum(v, -700.0)))


K, T, E, C, H, N = 1536, 1024, 8, 256, 512, 128


def by_expert(wq, xq):
    return np.concatenate([wq[e].T @ xq[:, e * C:(e + 1) * C] for e in range(E)], axis=1)


def setup_inputs():
    n = np.random.standard_normal
    s = mx_kscale(K)
    u = mx_kscale(H)
    first = np.random.permutation(np.repeat(np.arange(E), T // E))
    second = (first + 1 + np.random.permutation(np.repeat(np.arange(E - 1), -(-T // (E - 1)))[:T])) % E
    while np.bincount(second, minlength=E).max() != T // E:
        load = np.bincount(second, minlength=E); hi, lo = int(load.argmax()), int(load.argmin())
        t = np.flatnonzero((second == hi) & (first != lo))[0]; second[t] = lo
    slot_token = np.empty(E * C, np.int64); pos = np.empty((2, T), np.int64); fill = np.zeros(E, np.int64)
    place = np.stack([np.random.permutation(C) for _ in range(E)])
    for r, deal in enumerate((first, second)):
        for t in np.random.permutation(T):
            e = deal[t]; j = e * C + place[e, fill[e]]; fill[e] += 1; slot_token[j] = t; pos[r, t] = j
    g = np.random.uniform(0.2, 0.8, T)
    x = pack_weight(n((K, T)) * s[:, None], "e4m3")
    w1 = pack_weight(n((K, H)) / np.sqrt(K) / s[:, None] * u, "e2m1")
    w2 = [pack_weight(m, "e2m1") for m in n((E, H, N)) / np.sqrt(H) / u[None, :, None]]
    return {
        "x_words": x[0],
        "x_scales": x[1],
        "w1_words": w1[0],
        "w1_scales": w1[1],
        "w2_words": np.stack([m[0] for m in w2]),
        "w2_scales": np.stack([m[1] for m in w2]),
        "gate": np.stack([np.tile(g, (128, 1)), np.tile(1.0 - g, (128, 1))]).astype(np.float32),
        "offs": striped(slot_token),
        "pos1": striped(pos[0]),
        "pos2": striped(pos[1]),
    }


def reference(x_words, x_scales, w1_words, w1_scales, w2_words, w2_scales, gate, offs, pos1, pos2):
    w1 = unpack_weight(w1_words, w1_scales, "e2m1")
    w2 = np.stack([unpack_weight(w2_words[e], w2_scales[e], "e2m1") for e in range(E)])
    idx = unstriped(offs)
    x = unpack_weight(x_words, x_scales, "e4m3")
    h = silu(w1.T @ x)
    y = by_expert(w2, mxq(h[:, idx], 0, "e4m3"))
    out = sum(f64(gate[r, :1]) * y[:, unstriped(p)] for r, p in enumerate((pos1, pos2)))
    return out

@@ -1,0 +1,224 @@
+from contextlib import ExitStack
+
+import concourse.mybir as mybir
+
+K, T, E, C, H, N = 1536, 1024, 8, 256, 512, 128
+FLOPS = 2 * K * H * T + 2 * H * N * E * C
+
+F32 = mybir.dt.float32
+BF16 = mybir.dt.bfloat16
+I32 = mybir.dt.int32
+U32 = mybir.dt.uint32
+U16 = mybir.dt.uint16
+U8 = mybir.dt.uint8
+FP8X4 = mybir.dt.float8_e4m3fn_x4
+FP4X4 = mybir.dt.float4_e2m1fn_x4
+SILU = mybir.ActivationFunctionType.Silu
+MULT = mybir.AluOpType.mult
+ADD = mybir.AluOpType.add
+
+P = 128
+PASSES = K // 512
+S = E * C
+HALF = T // 2
+SLOT_CHUNKS = [512, 512, 512, 256, 128, 128]
+DIRECT_FROM = 4
+TOKEN_CHUNKS = [256, 256, 256, 128, 128]
+
+
+def starts(widths):
+    return [sum(widths[:i]) for i in range(len(widths))]
+
+
+def tile_moe_sup_lin_silu_kernel(
+    tc, x_words, x_scales, w1_words, w1_scales, w2_words, w2_scales, gate, offs, pos1, pos2, out
+):
+    nc = tc.nc
+    with ExitStack() as ctx:
+        keep = ctx.enter_context(tc.tile_pool(name="keep", bufs=1))
+        psum = ctx.enter_context(tc.psum_pool(name="psum", bufs=1))
+
+        def bank(b):
+            return psum.tile([P, 512], F32, name=f"bank{b}", tag=f"bank{b}")
+
+        w1w_raw = keep.tile([P, PASSES, 2 * H], U8, align_bytes=64)
+        w1s_raw = keep.tile([P, PASSES, H], U8, align_bytes=64)
+        xs = keep.tile([P, PASSES, T], U8, align_bytes=64)
+        w2w = keep.tile([P, E, 2 * N], U8, align_bytes=64)
+        w2s = keep.tile([P, E, N], U8, align_bytes=64)
+        warm_in = keep.tile([P, 8], F32)
+        warm_out = keep.tile([P, 8], F32)
+
+        nc.vector.memset(w1s_raw[:].bitcast(I32), 0)
+        nc.vector.memset(xs[:].bitcast(I32), 0)
+        nc.vector.memset(warm_in[:], 0.0)
+        nc.scalar.activation(warm_out[:], warm_in[:], SILU)
+        nc.vector.memset(w2s[:].bitcast(I32), 0)
+
+        nc.sync.dma_start(out=w1w_raw[:].bitcast(I32), in_=w1_words.rearrange("s p n -> p s n").bitcast(I32))
+        for q in range(4):
+            nc.sync.dma_start(
+                out=w1s_raw[32 * q : 32 * q + 4].bitcast(I32),
+                in_=w1_scales[:, 4 * q : 4 * q + 4, :].rearrange("s b n -> b s n").bitcast(I32),
+            )
+        for q in range(4):
+            nc.sync.dma_start(
+                out=xs[32 * q : 32 * q + 4].bitcast(I32),
+                in_=x_scales[:, 4 * q : 4 * q + 4, :].rearrange("s b n -> b s n").bitcast(I32),
+            )
+        xw = x_words.rearrange("s p t d -> p s (t d)").bitcast(I32)
+        x_lo = [keep.tile([P, HALF], I32, name=f"x_lo{s}", align_bytes=64) for s in range(PASSES)]
+        for s in range(PASSES):
+            nc.sync.dma_start(out=x_lo[s][:], in_=xw[:, s, 0:HALF])
+        x_up = keep.tile([P, PASSES, HALF], I32, align_bytes=64)
+        for j in range(2):
+            nc.sync.dma_start(
+                out=x_up[:, :, 256 * j : 256 * (j + 1)], in_=xw[:, :, HALF + 256 * j : HALF + 256 * (j + 1)]
+            )
+        slot_list = keep.tile([P, S // 16], U16)
+        nc.sync.dma_start(slot_list[:], offs)
+        nc.sync.dma_start(out=w2w[:].bitcast(I32), in_=w2_words.rearrange("e g p n -> p (e g) n").bitcast(I32))
+        for q in range(4):
+            nc.sync.dma_start(
+                out=w2s[32 * q : 32 * q + 4].bitcast(I32),
+                in_=w2_scales[:, 0, 4 * q : 4 * q + 4, :].rearrange("e b n -> b e n").bitcast(I32),
+            )
+        pos_a = keep.tile([P, T // 16], U16)
+        pos_b = keep.tile([P, T // 16], U16)
+        nc.sync.dma_start(pos_a[:], pos1)
+        nc.sync.dma_start(pos_b[:], pos2)
+        gates = keep.tile([P, 2, T], F32)
+        nc.sync.dma_start(out=gates[:], in_=gate.rearrange("r p t -> p r t"))
+
+        w1w = [keep.tile([P, 2, PASSES, 2 * P], U8, name=f"w1w{u}", align_bytes=64) for u in range(2)]
+        w1s = [keep.tile([P, 2, PASSES, P], U8, name=f"w1s{u}", align_bytes=64) for u in range(2)]
+        for u in range(2):
+            nc.vector.tensor_copy(
+                out=w1w[u][:].bitcast(U16),
+                in_=w1w_raw[:].bitcast(U16).rearrange("p s (m t) -> p t s m", t=4)[:, 2 * u : 2 * u + 2],
+            )
+            nc.vector.tensor_copy(
+                out=w1s[u][:],
+                in_=w1s_raw[:].rearrange("p s (m t) -> p t s m", t=4)[:, 2 * u : 2 * u + 2],
+            )
+
+        h = [keep.tile([P, T], U32, name=f"h{u}", align_bytes=64) for u in range(2)]
+
+        def h_view(u):
+            return h[u][:].bitcast(BF16).rearrange("p (t e) -> p t e", e=2)
+
+        def first_layer(acc, u, e, t0, width):
+            for s in range(PASSES):
+                if t0 < HALF:
+                    rhs = x_lo[s][:, t0 : t0 + width]
+                else:
+                    rhs = x_up[:, s, t0 - HALF : t0 - HALF + width]
+                nc.tensor.matmul_mx(
+                    out=acc,
+                    lhsT=w1w[u][:, e, s, :].bitcast(FP4X4),
+                    lhsT_scale=w1s[u][:, e, s, :],
+                    rhs=rhs.bitcast(FP8X4),
+                    rhs_scale=xs[:, s, t0 : t0 + width],
+                    start=(s == 0),
+                    stop=(s == PASSES - 1),
+                )
+
+        def wide(b, u, e, t0):
+            acc = bank(b)
+            first_layer(acc[:], u, e, t0, HALF)
+            nc.scalar.activation(h_view(u)[:, t0 : t0 + HALF, e], acc[:], SILU)
+
+        def narrow(b, u, t0):
+            acc = bank(b)
+            for e in range(2):
+                first_layer(acc[:, P * e : P * (e + 1)], u, e, t0, P)
+            nc.scalar.activation(
+                h_view(u)[:, t0 : t0 + P, :], acc[:, 0 : 2 * P].rearrange("p (e t) -> p t e", e=2), SILU
+            )
+
+        wide(0, 0, 0, 0)
+        wide(1, 0, 1, 0)
+        for j in range(4):
+            narrow(2 + j, 0, HALF + P * j)
+        for j in range(4):
+            wide(4 + j % 2, 1, j % 2, HALF * (j // 2))
+
+        y = keep.tile([P, S], F32)
+        s0 = starts(SLOT_CHUNKS)
+        nchunks = len(SLOT_CHUNKS)
+        grouped = [keep.tile([P, 4 * w], BF16, name=f"grouped{c}", align_bytes=64) for c, w in enumerate(SLOT_CHUNKS)]
+        pairs = [keep.tile([P, 2, w], U32, name=f"pairs{c}") for c, w in enumerate(SLOT_CHUNKS[:DIRECT_FROM])]
+        codes = [keep.tile([P, w], U32, name=f"codes{c}", align_bytes=64) for c, w in enumerate(SLOT_CHUNKS)]
+        scales = [keep.tile([P, w], U8, name=f"scales{c}", align_bytes=64) for c, w in enumerate(SLOT_CHUNKS)]
+        second_banks = [0, 1, 6, 7, 2, 3]
+
+        def gather(c, u):
+            w = SLOT_CHUNKS[c]
+            src = h[u][:].indirect(slot_list[:, s0[c] // 16 : (s0[c] + w) // 16])
+            if c < DIRECT_FROM:
+                dst = pairs[c][:, u, :]
+            else:
+                dst = grouped[c][:].bitcast(U32).rearrange("p (n u) -> p n u", u=2)[:, :, u]
+            nc.vector.tensor_copy(dst, src)
+
+        def interleave(c):
+            if c < DIRECT_FROM:
+                nc.scalar.copy(
+                    out=grouped[c][:].bitcast(F32).rearrange("p (n u) -> p n u", u=2),
+                    in_=pairs[c][:].bitcast(F32).rearrange("p u n -> p n u"),
+                )
+
+        def second_layer(c):
+            w = SLOT_CHUNKS[c]
+            nc.vector.quantize_mx(out=codes[c][:].bitcast(FP8X4), scales=scales[c][:], in_=grouped[c][:])
+            acc = bank(second_banks[c])
+            step = min(w, C)
+            for a in range(0, w, step):
+                e = (s0[c] + a) // C
+                nc.tensor.matmul_mx(
+                    out=acc[:, a : a + step],
+                    lhsT=w2w[:, e, :].bitcast(FP4X4),
+                    lhsT_scale=w2s[:, e, :],
+                    rhs=codes[c][:, a : a + step].bitcast(FP8X4),
+                    rhs_scale=scales[c][:, a : a + step],
+                    start=True,
+                    stop=True,
+                )
+            nc.scalar.copy(out=y[:, s0[c] : s0[c] + w], in_=acc[:, 0:w])
+
+        for c in range(nchunks):
+            gather(c, 0)
+        for c in range(nchunks + 1):
+            if c < nchunks:
+                gather(c, 1)
+                interleave(c)
+            if c >= 1:
+                second_layer(c - 1)
+
+        t0 = starts(TOKEN_CHUNKS)
+        ntok = len(TOKEN_CHUNKS)
+        terms = [keep.tile([P, 2, w], F32, name=f"terms{c}") for c, w in enumerate(TOKEN_CHUNKS)]
+        sums = [keep.tile([P, w], F32, name=f"sums{c}") for c, w in enumerate(TOKEN_CHUNKS)]
+
+        def fetch(c, r):
+            w = TOKEN_CHUNKS[c]
+            lst = (pos_a, pos_b)[r]
+            nc.vector.tensor_tensor(
+                terms[c][:, r, :],
+                y[:].indirect(lst[:, t0[c] // 16 : (t0[c] + w) // 16]),
+                gates[:, r, t0[c] : t0[c] + w],
+                MULT,
+            )
+
+        def finish(c):
+            w = TOKEN_CHUNKS[c]
+            nc.vector.tensor_tensor(sums[c][:], terms[c][:, 0, :], terms[c][:, 1, :], ADD)
+            nc.sync.dma_start(out=out[:, t0[c] : t0[c] + w], in_=sums[c][:])
+
+        for c in range(ntok + 1):
+            if c < ntok:
+                fetch(c, 0)
+            if c >= 1:
+                finish(c - 1)
+            if c < ntok:
+                fetch(c, 1)

@@ -1,6 +1,7 @@
 from contextlib import ExitStack
 
 import concourse.mybir as mybir
+from concourse.masks import make_identity
 
 K, T, E, C, H, N = 1536, 1024, 8, 256, 512, 128
 FLOPS = 2 * K * H * T + 2 * H * N * E * C
@@ -21,8 +22,9 @@ P = 128
 PASSES = K // 512
 S = E * C
 HALF = T // 2
-SLOT_CHUNKS = [512, 512, 512, 256, 128, 128]
-DIRECT_FROM = 4
+SLOT_CHUNKS = [256, 512, 512, 256, 256, 128, 128]
+DIRECT_FROM = 5
+WARM_TRANSPOSES = 24
 TOKEN_CHUNKS = [256, 256, 256, 128, 128]
 
 
@@ -49,6 +51,14 @@ def tile_moe_sup_lin_silu_kernel(
         warm_in = keep.tile([P, 8], F32)
         warm_out = keep.tile([P, 8], F32)
 
+        xw = x_words.rearrange("s p t d -> p s (t d)").bitcast(I32)
+        x_lo = [keep.tile([P, HALF], I32, name=f"x_lo{s}", align_bytes=64) for s in range(PASSES)]
+        ident = keep.tile([P, P], BF16)
+        make_identity(nc, ident[:])
+        scratch = psum.tile([P, 4, P], BF16, name="bank7", tag="bank7")
+        for j in range(WARM_TRANSPOSES):
+            nc.tensor.transpose(scratch[:, j % 4, :], ident[:], ident[:])
+
         nc.vector.memset(w1s_raw[:].bitcast(I32), 0)
         nc.vector.memset(xs[:].bitcast(I32), 0)
         nc.vector.memset(warm_in[:], 0.0)
@@ -56,19 +66,24 @@ def tile_moe_sup_lin_silu_kernel(
         nc.vector.memset(w2s[:].bitcast(I32), 0)
 
         nc.sync.dma_start(out=w1w_raw[:].bitcast(I32), in_=w1_words.rearrange("s p n -> p s n").bitcast(I32))
-        for q in range(4):
+        for q in (0, 2, 1, 3):
             nc.sync.dma_start(
                 out=w1s_raw[32 * q : 32 * q + 4].bitcast(I32),
                 in_=w1_scales[:, 4 * q : 4 * q + 4, :].rearrange("s b n -> b s n").bitcast(I32),
             )
-        for q in range(4):
+
+        def load_xs(q):
             nc.sync.dma_start(
                 out=xs[32 * q : 32 * q + 4].bitcast(I32),
                 in_=x_scales[:, 4 * q : 4 * q + 4, :].rearrange("s b n -> b s n").bitcast(I32),
             )
-        xw = x_words.rearrange("s p t d -> p s (t d)").bitcast(I32)
-        x_lo = [keep.tile([P, HALF], I32, name=f"x_lo{s}", align_bytes=64) for s in range(PASSES)]
-        for s in range(PASSES):
+
+        load_xs(0)
+        load_xs(2)
+        nc.sync.dma_start(out=x_lo[0][:], in_=xw[:, 0, 0:HALF])
+        load_xs(1)
+        load_xs(3)
+        for s in range(1, PASSES):
             nc.sync.dma_start(out=x_lo[s][:], in_=xw[:, s, 0:HALF])
         x_up = keep.tile([P, PASSES, HALF], I32, align_bytes=64)
         for j in range(2):
@@ -150,7 +165,7 @@ def tile_moe_sup_lin_silu_kernel(
         pairs = [keep.tile([P, 2, w], U32, name=f"pairs{c}") for c, w in enumerate(SLOT_CHUNKS[:DIRECT_FROM])]
         codes = [keep.tile([P, w], U32, name=f"codes{c}", align_bytes=64) for c, w in enumerate(SLOT_CHUNKS)]
         scales = [keep.tile([P, w], U8, name=f"scales{c}", align_bytes=64) for c, w in enumerate(SLOT_CHUNKS)]
-        second_banks = [0, 1, 6, 7, 2, 3]
+        second_banks = [0, 1, 6, 7, 2, 3, 0]
 
         def gather(c, u):
             w = SLOT_CHUNKS[c]
@@ -184,16 +199,19 @@ def tile_moe_sup_lin_silu_kernel(
                     start=True,
                     stop=True,
                 )
-            nc.scalar.copy(out=y[:, s0[c] : s0[c] + w], in_=acc[:, 0:w])
+            if c == nchunks - 1:
+                nc.vector.tensor_copy(out=y[:, s0[c] : s0[c] + w], in_=acc[:, 0:w])
+            else:
+                nc.scalar.copy(out=y[:, s0[c] : s0[c] + w], in_=acc[:, 0:w])
 
         for c in range(nchunks):
             gather(c, 0)
-        for c in range(nchunks + 1):
+        for c in range(nchunks + 2):
             if c < nchunks:
                 gather(c, 1)
                 interleave(c)
-            if c >= 1:
-                second_layer(c - 1)
+            if c >= 2:
+                second_layer(c - 2)
 
         t0 = starts(TOKEN_CHUNKS)
         ntok = len(TOKEN_CHUNKS)

@@ -1,7 +1,6 @@
 from contextlib import ExitStack
 
 import concourse.mybir as mybir
-from concourse.masks import make_identity
 
 K, T, E, C, H, N = 1536, 1024, 8, 256, 512, 128
 FLOPS = 2 * K * H * T + 2 * H * N * E * C
@@ -24,7 +23,7 @@ S = E * C
 HALF = T // 2
 SLOT_CHUNKS = [256, 512, 512, 256, 256, 128, 128]
 DIRECT_FROM = 5
-WARM_TRANSPOSES = 24
+WARM_PASSES = 11
 TOKEN_CHUNKS = [256, 256, 256, 128, 128]
 
 
@@ -53,12 +52,6 @@ def tile_moe_sup_lin_silu_kernel(
 
         xw = x_words.rearrange("s p t d -> p s (t d)").bitcast(I32)
         x_lo = [keep.tile([P, HALF], I32, name=f"x_lo{s}", align_bytes=64) for s in range(PASSES)]
-        ident = keep.tile([P, P], BF16)
-        make_identity(nc, ident[:])
-        scratch = psum.tile([P, 4, P], BF16, name="bank7", tag="bank7")
-        for j in range(WARM_TRANSPOSES):
-            nc.tensor.transpose(scratch[:, j % 4, :], ident[:], ident[:])
-
         nc.vector.memset(w1s_raw[:].bitcast(I32), 0)
         nc.vector.memset(xs[:].bitcast(I32), 0)
         nc.vector.memset(warm_in[:], 0.0)
@@ -104,6 +97,23 @@ def tile_moe_sup_lin_silu_kernel(
         nc.sync.dma_start(pos_b[:], pos2)
         gates = keep.tile([P, 2, T], F32)
         nc.sync.dma_start(out=gates[:], in_=gate.rearrange("r p t -> p r t"))
+
+        zeros = keep.tile([P, 4 * P], BF16, align_bytes=64)
+        zero_codes = keep.tile([P, P], U32, align_bytes=64)
+        zero_scales = keep.tile([P, P], U8, align_bytes=64)
+        nc.vector.memset(zeros[:], 0.0)
+        nc.vector.quantize_mx(out=zero_codes[:].bitcast(FP8X4), scales=zero_scales[:], in_=zeros[:])
+        scratch = bank(7)
+        for j in range(WARM_PASSES):
+            nc.tensor.matmul_mx(
+                out=scratch[:, P * (j % 4) : P * (j % 4 + 1)],
+                lhsT=w1w_raw[:, 0, 0 : 2 * P].bitcast(FP4X4),
+                lhsT_scale=zero_scales[:],
+                rhs=zero_codes[:].bitcast(FP8X4),
+                rhs_scale=zero_scales[:],
+                start=True,
+                stop=True,
+            )
 
         w1w = [keep.tile([P, 2, PASSES, 2 * P], U8, name=f"w1w{u}", align_bytes=64) for u in range(2)]
         w1s = [keep.tile([P, 2, PASSES, P], U8, name=f"w1s{u}", align_bytes=64) for u in range(2)]
@@ -156,7 +166,7 @@ def tile_moe_sup_lin_silu_kernel(
         for j in range(4):
             narrow(2 + j, 0, HALF + P * j)
         for j in range(4):
-            wide(4 + j % 2, 1, j % 2, HALF * (j // 2))
+            wide(2 + j, 1, j % 2, HALF * (1 - j // 2))
 
         y = keep.tile([P, S], F32)
         s0 = starts(SLOT_CHUNKS)

@@ -1,6 +1,7 @@
 from contextlib import ExitStack
 
 import concourse.mybir as mybir
+from concourse.masks import make_identity
 
 K, T, E, C, H, N = 1536, 1024, 8, 256, 512, 128
 FLOPS = 2 * K * H * T + 2 * H * N * E * C
@@ -22,9 +23,10 @@ PASSES = K // 512
 S = E * C
 HALF = T // 2
 SLOT_CHUNKS = [256, 512, 512, 256, 256, 128, 128]
-DIRECT_FROM = 5
+DIRECT_FROM = 6
 WARM_PASSES = 11
 TOKEN_CHUNKS = [256, 256, 256, 128, 128]
+TENSOR_ADDS = 2
 
 
 def starts(widths):
@@ -52,6 +54,8 @@ def tile_moe_sup_lin_silu_kernel(
 
         xw = x_words.rearrange("s p t d -> p s (t d)").bitcast(I32)
         x_lo = [keep.tile([P, HALF], I32, name=f"x_lo{s}", align_bytes=64) for s in range(PASSES)]
+        ident = keep.tile([P, P], F32)
+        make_identity(nc, ident[:])
         nc.vector.memset(w1s_raw[:].bitcast(I32), 0)
         nc.vector.memset(xs[:].bitcast(I32), 0)
         nc.vector.memset(warm_in[:], 0.0)
@@ -240,8 +244,28 @@ def tile_moe_sup_lin_silu_kernel(
 
         def finish(c):
             w = TOKEN_CHUNKS[c]
-            nc.vector.tensor_tensor(sums[c][:], terms[c][:, 0, :], terms[c][:, 1, :], ADD)
-            nc.sync.dma_start(out=out[:, t0[c] : t0[c] + w], in_=sums[c][:])
+            if c < TENSOR_ADDS:
+                turned = bank(4 + c)
+                for a in range(0, w, P):
+                    for r in range(2):
+                        nc.tensor.matmul(
+                            turned[:, a : a + P],
+                            terms[c][:, r, a : a + P],
+                            ident[:],
+                            start=(r == 0),
+                            stop=(r == 1),
+                            is_transpose=True,
+                        )
+                by_token = keep.tile([P, w], F32, name=f"by_token{c}")
+                nc.scalar.copy(out=by_token[:], in_=turned[:, 0:w])
+                back = bank(6 + c)
+                for a in range(0, w, P):
+                    nc.tensor.transpose(back[:, a : a + P], by_token[:, a : a + P], ident[:])
+                nc.scalar.copy(out=sums[c][:], in_=back[:, 0:w])
+            else:
+                nc.vector.tensor_tensor(sums[c][:], terms[c][:, 0, :], terms[c][:, 1, :], ADD)
+            queue = nc.scalar if c < TENSOR_ADDS else nc.sync
+            queue.dma_start(out=out[:, t0[c] : t0[c] + w], in_=sums[c][:])
 
         for c in range(ntok + 1):
             if c < ntok:

@@ -23,9 +23,9 @@ PASSES = K // 512
 S = E * C
 HALF = T // 2
 SLOT_CHUNKS = [256, 512, 512, 256, 256, 128, 128]
-DIRECT_FROM = 6
+DIRECT_FROM = 5
 WARM_PASSES = 11
-TOKEN_CHUNKS = [256, 256, 256, 128, 128]
+TOKEN_CHUNKS = [256, 128, 256, 256, 128]
 TENSOR_ADDS = 2
 
 
@@ -45,21 +45,15 @@ def tile_moe_sup_lin_silu_kernel(
             return psum.tile([P, 512], F32, name=f"bank{b}", tag=f"bank{b}")
 
         w1w_raw = keep.tile([P, PASSES, 2 * H], U8, align_bytes=64)
-        w1s_raw = keep.tile([P, PASSES, H], U8, align_bytes=64)
+        w1s_raw = keep.tile([P, PASSES, H], U8, tag="w1s_raw", align_bytes=64)
         xs = keep.tile([P, PASSES, T], U8, align_bytes=64)
         w2w = keep.tile([P, E, 2 * N], U8, align_bytes=64)
         w2s = keep.tile([P, E, N], U8, align_bytes=64)
-        warm_in = keep.tile([P, 8], F32)
-        warm_out = keep.tile([P, 8], F32)
 
         xw = x_words.rearrange("s p t d -> p s (t d)").bitcast(I32)
         x_lo = [keep.tile([P, HALF], I32, name=f"x_lo{s}", align_bytes=64) for s in range(PASSES)]
-        ident = keep.tile([P, P], F32)
-        make_identity(nc, ident[:])
         nc.vector.memset(w1s_raw[:].bitcast(I32), 0)
         nc.vector.memset(xs[:].bitcast(I32), 0)
-        nc.vector.memset(warm_in[:], 0.0)
-        nc.scalar.activation(warm_out[:], warm_in[:], SILU)
         nc.vector.memset(w2s[:].bitcast(I32), 0)
 
         nc.sync.dma_start(out=w1w_raw[:].bitcast(I32), in_=w1_words.rearrange("s p n -> p s n").bitcast(I32))
@@ -130,6 +124,9 @@ def tile_moe_sup_lin_silu_kernel(
                 out=w1s[u][:],
                 in_=w1s_raw[:].rearrange("p s (m t) -> p t s m", t=4)[:, 2 * u : 2 * u + 2],
             )
+
+        ident = keep.tile([P, P], F32, name="ident", tag="w1s_raw", align_bytes=64)
+        make_identity(nc, ident[:])
 
         h = [keep.tile([P, T], U32, name=f"h{u}", align_bytes=64) for u in range(2)]
 

@@ -15,6 +15,7 @@ U8 = mybir.dt.uint8
 FP8X4 = mybir.dt.float8_e4m3fn_x4
 FP4X4 = mybir.dt.float4_e2m1fn_x4
 SILU = mybir.ActivationFunctionType.Silu
+COPY = mybir.ActivationFunctionType.Copy
 MULT = mybir.AluOpType.mult
 ADD = mybir.AluOpType.add
 
@@ -22,11 +23,13 @@ P = 128
 PASSES = K // 512
 S = E * C
 HALF = T // 2
-SLOT_CHUNKS = [256, 512, 512, 256, 256, 128, 128]
-DIRECT_FROM = 5
-WARM_PASSES = 11
-TOKEN_CHUNKS = [256, 128, 256, 256, 128]
-TENSOR_ADDS = 2
+SLOT_CHUNKS = [512, 512, 512, 256, 128, 128]
+WARM_WIDTHS = [512, 512, 256]
+FIRST_GATHERS = [768, 768, 512]
+SECOND_GATHERS = [512, 512, 512, 256, 256]
+PLAIN_FETCHES = [256, 384]
+TURNED_UNITS = [2, 2, 1]
+DIRECT_CHUNKS = [256, 128]
 
 
 def starts(widths):
@@ -51,50 +54,31 @@ def tile_moe_sup_lin_silu_kernel(
         w2s = keep.tile([P, E, N], U8, align_bytes=64)
 
         xw = x_words.rearrange("s p t d -> p s (t d)").bitcast(I32)
-        x_lo = [keep.tile([P, HALF], I32, name=f"x_lo{s}", align_bytes=64) for s in range(PASSES)]
         nc.vector.memset(w1s_raw[:].bitcast(I32), 0)
         nc.vector.memset(xs[:].bitcast(I32), 0)
-        nc.vector.memset(w2s[:].bitcast(I32), 0)
 
         nc.sync.dma_start(out=w1w_raw[:].bitcast(I32), in_=w1_words.rearrange("s p n -> p s n").bitcast(I32))
-        for q in (0, 2, 1, 3):
+
+        def load_scale_rows(plane, source, r):
             nc.sync.dma_start(
-                out=w1s_raw[32 * q : 32 * q + 4].bitcast(I32),
-                in_=w1_scales[:, 4 * q : 4 * q + 4, :].rearrange("s b n -> b s n").bitcast(I32),
+                out=plane[r:P:32].bitcast(I32), in_=source[:, r:16:4, :].rearrange("s b n -> b s n").bitcast(I32)
             )
 
-        def load_xs(q):
-            nc.sync.dma_start(
-                out=xs[32 * q : 32 * q + 4].bitcast(I32),
-                in_=x_scales[:, 4 * q : 4 * q + 4, :].rearrange("s b n -> b s n").bitcast(I32),
-            )
-
-        load_xs(0)
-        load_xs(2)
+        for r in range(4):
+            load_scale_rows(w1s_raw, w1_scales, r)
+        x_lo = [keep.tile([P, HALF], I32, name=f"x_lo{s}", align_bytes=64) for s in range(PASSES)]
+        x_up = [keep.tile([P, PASSES, 256], I32, name=f"x_up{j}", align_bytes=64) for j in range(2)]
+        load_scale_rows(xs, x_scales, 0)
+        load_scale_rows(xs, x_scales, 1)
         nc.sync.dma_start(out=x_lo[0][:], in_=xw[:, 0, 0:HALF])
-        load_xs(1)
-        load_xs(3)
+        load_scale_rows(xs, x_scales, 2)
+        load_scale_rows(xs, x_scales, 3)
         for s in range(1, PASSES):
             nc.sync.dma_start(out=x_lo[s][:], in_=xw[:, s, 0:HALF])
-        x_up = keep.tile([P, PASSES, HALF], I32, align_bytes=64)
         for j in range(2):
-            nc.sync.dma_start(
-                out=x_up[:, :, 256 * j : 256 * (j + 1)], in_=xw[:, :, HALF + 256 * j : HALF + 256 * (j + 1)]
-            )
+            nc.sync.dma_start(out=x_up[j][:], in_=xw[:, :, HALF + 256 * j : HALF + 256 * (j + 1)])
         slot_list = keep.tile([P, S // 16], U16)
         nc.sync.dma_start(slot_list[:], offs)
-        nc.sync.dma_start(out=w2w[:].bitcast(I32), in_=w2_words.rearrange("e g p n -> p (e g) n").bitcast(I32))
-        for q in range(4):
-            nc.sync.dma_start(
-                out=w2s[32 * q : 32 * q + 4].bitcast(I32),
-                in_=w2_scales[:, 0, 4 * q : 4 * q + 4, :].rearrange("e b n -> b e n").bitcast(I32),
-            )
-        pos_a = keep.tile([P, T // 16], U16)
-        pos_b = keep.tile([P, T // 16], U16)
-        nc.sync.dma_start(pos_a[:], pos1)
-        nc.sync.dma_start(pos_b[:], pos2)
-        gates = keep.tile([P, 2, T], F32)
-        nc.sync.dma_start(out=gates[:], in_=gate.rearrange("r p t -> p r t"))
 
         zeros = keep.tile([P, 4 * P], BF16, align_bytes=64)
         zero_codes = keep.tile([P, P], U32, align_bytes=64)
@@ -102,13 +86,13 @@ def tile_moe_sup_lin_silu_kernel(
         nc.vector.memset(zeros[:], 0.0)
         nc.vector.quantize_mx(out=zero_codes[:].bitcast(FP8X4), scales=zero_scales[:], in_=zeros[:])
         scratch = bank(7)
-        for j in range(WARM_PASSES):
+        for s, w in enumerate(WARM_WIDTHS):
             nc.tensor.matmul_mx(
-                out=scratch[:, P * (j % 4) : P * (j % 4 + 1)],
-                lhsT=w1w_raw[:, 0, 0 : 2 * P].bitcast(FP4X4),
+                out=scratch[:, 0:w],
+                lhsT=zero_codes[:].bitcast(FP8X4),
                 lhsT_scale=zero_scales[:],
-                rhs=zero_codes[:].bitcast(FP8X4),
-                rhs_scale=zero_scales[:],
+                rhs=w1w_raw[:, s, 0 : 2 * w].bitcast(FP4X4),
+                rhs_scale=w1s_raw[:, s, 0:w],
                 start=True,
                 stop=True,
             )
@@ -125,6 +109,25 @@ def tile_moe_sup_lin_silu_kernel(
                 in_=w1s_raw[:].rearrange("p s (m t) -> p t s m", t=4)[:, 2 * u : 2 * u + 2],
             )
 
+        nc.vector.memset(w2s[:].bitcast(I32), 0)
+        nc.sync.dma_start(out=w2w[:].bitcast(I32), in_=w2_words.rearrange("e g p n -> p (e g) n").bitcast(I32))
+        for r in range(4):
+            load_scale_rows(w2s, w2_scales.rearrange("e g b n -> (e g) b n"), r)
+        pos_a = keep.tile([P, T // 16], U16)
+        pos_b = keep.tile([P, T // 16], U16)
+        nc.sync.dma_start(pos_a[:], pos1)
+        nc.sync.dma_start(pos_b[:], pos2)
+        turned_tokens = sum(PLAIN_FETCHES)
+        blocks = T // P
+        gate_rows = keep.tile([P, P], F32)
+        nc.vector.memset(gate_rows[:], 0.0)
+        for r in range(2):
+            nc.sync.dma_start(
+                out=gate_rows[blocks * r : blocks * (r + 1), :], in_=gate[r, 0, :].rearrange("(b t) -> b t", t=P)
+            )
+        gates = keep.tile([P, 2, T - turned_tokens], F32)
+        nc.sync.dma_start(out=gates[:], in_=gate[:, :, turned_tokens:T].rearrange("r p t -> p r t"))
+
         ident = keep.tile([P, P], F32, name="ident", tag="w1s_raw", align_bytes=64)
         make_identity(nc, ident[:])
 
@@ -138,7 +141,8 @@ def tile_moe_sup_lin_silu_kernel(
                 if t0 < HALF:
                     rhs = x_lo[s][:, t0 : t0 + width]
                 else:
-                    rhs = x_up[:, s, t0 - HALF : t0 - HALF + width]
+                    j, a = divmod(t0 - HALF, 256)
+                    rhs = x_up[j][:, s, a : a + width]
                 nc.tensor.matmul_mx(
                     out=acc,
                     lhsT=w1w[u][:, e, s, :].bitcast(FP4X4),
@@ -154,120 +158,160 @@ def tile_moe_sup_lin_silu_kernel(
             first_layer(acc[:], u, e, t0, HALF)
             nc.scalar.activation(h_view(u)[:, t0 : t0 + HALF, e], acc[:], SILU)
 
-        def narrow(b, u, t0):
+        def narrow(b, u, t0, groups):
             acc = bank(b)
-            for e in range(2):
-                first_layer(acc[:, P * e : P * (e + 1)], u, e, t0, P)
+            for j in range(groups):
+                for e in range(2):
+                    first_layer(acc[:, P * (2 * j + e) : P * (2 * j + e + 1)], u, e, t0 + P * j, P)
             nc.scalar.activation(
-                h_view(u)[:, t0 : t0 + P, :], acc[:, 0 : 2 * P].rearrange("p (e t) -> p t e", e=2), SILU
+                h_view(u)[:, t0 : t0 + P * groups, :].rearrange("p (j t) e -> p j t e", t=P),
+                acc[:, 0 : 2 * P * groups].rearrange("p (j e t) -> p j t e", e=2, t=P),
+                SILU,
             )
 
         wide(0, 0, 0, 0)
         wide(1, 0, 1, 0)
-        for j in range(4):
-            narrow(2 + j, 0, HALF + P * j)
-        for j in range(4):
-            wide(2 + j, 1, j % 2, HALF * (1 - j // 2))
+        narrow(2, 0, HALF, 2)
+        narrow(3, 0, HALF + 2 * P, 1)
+        narrow(4, 0, HALF + 3 * P, 1)
+        wide(3, 1, 0, 0)
+        wide(4, 1, 1, 0)
+        narrow(3, 1, HALF, 2)
+        narrow(4, 1, HALF + 2 * P, 2)
+
+        gate_bank = bank(4)
+        nc.tensor.transpose(gate_bank[:, 0:P], gate_rows[:], ident[:])
+        gate_cols = keep.tile([P, 2 * blocks], F32)
+        nc.scalar.copy(out=gate_cols[:], in_=gate_bank[:, 0 : 2 * blocks])
 
         y = keep.tile([P, S], F32)
-        s0 = starts(SLOT_CHUNKS)
-        nchunks = len(SLOT_CHUNKS)
-        grouped = [keep.tile([P, 4 * w], BF16, name=f"grouped{c}", align_bytes=64) for c, w in enumerate(SLOT_CHUNKS)]
-        pairs = [keep.tile([P, 2, w], U32, name=f"pairs{c}") for c, w in enumerate(SLOT_CHUNKS[:DIRECT_FROM])]
-        codes = [keep.tile([P, w], U32, name=f"codes{c}", align_bytes=64) for c, w in enumerate(SLOT_CHUNKS)]
-        scales = [keep.tile([P, w], U8, name=f"scales{c}", align_bytes=64) for c, w in enumerate(SLOT_CHUNKS)]
-        second_banks = [0, 1, 6, 7, 2, 3, 0]
+        pairs = keep.tile([P, 2, S], U32)
+        grouped = keep.tile([P, 4 * S], BF16, align_bytes=64)
+        codes = keep.tile([P, S], U32, align_bytes=64)
+        scales = keep.tile([P, S], U8, align_bytes=64)
 
-        def gather(c, u):
-            w = SLOT_CHUNKS[c]
-            src = h[u][:].indirect(slot_list[:, s0[c] // 16 : (s0[c] + w) // 16])
-            if c < DIRECT_FROM:
-                dst = pairs[c][:, u, :]
-            else:
-                dst = grouped[c][:].bitcast(U32).rearrange("p (n u) -> p n u", u=2)[:, :, u]
-            nc.vector.tensor_copy(dst, src)
+        def gather(u, a, w):
+            nc.vector.tensor_copy(pairs[:, u, a : a + w], h[u][:].indirect(slot_list[:, a // 16 : (a + w) // 16]))
 
-        def interleave(c):
-            if c < DIRECT_FROM:
-                nc.scalar.copy(
-                    out=grouped[c][:].bitcast(F32).rearrange("p (n u) -> p n u", u=2),
-                    in_=pairs[c][:].bitcast(F32).rearrange("p u n -> p n u"),
-                )
+        def interleave(a, w):
+            nc.scalar.copy(
+                out=grouped[:, 4 * a : 4 * (a + w)].bitcast(U32).rearrange("p (n u) -> p n u", u=2),
+                in_=pairs[:, :, a : a + w].rearrange("p u n -> p n u"),
+            )
 
-        def second_layer(c):
-            w = SLOT_CHUNKS[c]
-            nc.vector.quantize_mx(out=codes[c][:].bitcast(FP8X4), scales=scales[c][:], in_=grouped[c][:])
-            acc = bank(second_banks[c])
+        def second_layer(c, a, w):
+            nc.vector.quantize_mx(
+                out=codes[:, a : a + w].bitcast(FP8X4), scales=scales[:, a : a + w], in_=grouped[:, 4 * a : 4 * (a + w)]
+            )
+            acc = bank((2, 5, 6, 7)[c % 4])
             step = min(w, C)
-            for a in range(0, w, step):
-                e = (s0[c] + a) // C
+            for j in range(0, w, step):
+                e = (a + j) // C
                 nc.tensor.matmul_mx(
-                    out=acc[:, a : a + step],
+                    out=acc[:, j : j + step],
                     lhsT=w2w[:, e, :].bitcast(FP4X4),
                     lhsT_scale=w2s[:, e, :],
-                    rhs=codes[c][:, a : a + step].bitcast(FP8X4),
-                    rhs_scale=scales[c][:, a : a + step],
+                    rhs=codes[:, a + j : a + j + step].bitcast(FP8X4),
+                    rhs_scale=scales[:, a + j : a + j + step],
                     start=True,
                     stop=True,
                 )
-            if c == nchunks - 1:
-                nc.vector.tensor_copy(out=y[:, s0[c] : s0[c] + w], in_=acc[:, 0:w])
+            if a + w == S:
+                nc.vector.tensor_copy(out=y[:, a : a + w], in_=acc[:, 0:w])
             else:
-                nc.scalar.copy(out=y[:, s0[c] : s0[c] + w], in_=acc[:, 0:w])
+                nc.scalar.copy(out=y[:, a : a + w], in_=acc[:, 0:w])
 
-        for c in range(nchunks):
-            gather(c, 0)
-        for c in range(nchunks + 2):
-            if c < nchunks:
-                gather(c, 1)
-                interleave(c)
-            if c >= 2:
-                second_layer(c - 2)
+        for a, w in zip(starts(FIRST_GATHERS), FIRST_GATHERS):
+            gather(0, a, w)
+        for a, w in zip(starts(SECOND_GATHERS), SECOND_GATHERS):
+            gather(1, a, w)
+            interleave(a, w)
+        for c, (a, w) in enumerate(zip(starts(SLOT_CHUNKS), SLOT_CHUNKS)):
+            second_layer(c, a, w)
 
-        t0 = starts(TOKEN_CHUNKS)
-        ntok = len(TOKEN_CHUNKS)
-        terms = [keep.tile([P, 2, w], F32, name=f"terms{c}") for c, w in enumerate(TOKEN_CHUNKS)]
-        sums = [keep.tile([P, w], F32, name=f"sums{c}") for c, w in enumerate(TOKEN_CHUNKS)]
+        lists = (pos_a, pos_b)
+        fetched = {}
+        weighted = {}
+        u0 = starts(TURNED_UNITS)
+        turned = {}
 
-        def fetch(c, r):
-            w = TOKEN_CHUNKS[c]
-            lst = (pos_a, pos_b)[r]
+        def fetch_plain(t, w):
+            for r in range(2):
+                got = keep.tile([P, w], F32, name=f"fetched{t}_{r}")
+                nc.vector.tensor_copy(got[:], y[:].indirect(lists[r][:, t // 16 : (t + w) // 16]))
+                for a in range(0, w, P):
+                    fetched[(r, t + a)] = got[:, a : a + P]
+
+        def turn(c):
+            turned[c] = bank(c % 2)
+            for r in range(2):
+                for b in range(TURNED_UNITS[c]):
+                    col = P * (2 * r + b)
+                    t = P * (u0[c] + b)
+                    nc.tensor.transpose(turned[c][:, col : col + P], fetched[(r, t)], ident[:])
+
+        def weigh(c):
+            for r in range(2):
+                for b in range(TURNED_UNITS[c]):
+                    col = P * (2 * r + b)
+                    t = P * (u0[c] + b)
+                    g = blocks * r + u0[c] + b
+                    weighted[(r, t)] = keep.tile([P, P], F32, name=f"weighted{t}_{r}")
+                    nc.scalar.activation(
+                        weighted[(r, t)][:], turned[c][:, col : col + P], COPY, scale=gate_cols[:, g : g + 1]
+                    )
+
+        def turn_back(c):
+            back = bank(3 + c % 2)
+            w = P * TURNED_UNITS[c]
+            for b in range(TURNED_UNITS[c]):
+                t = P * (u0[c] + b)
+                for r in range(2):
+                    nc.tensor.matmul(
+                        back[:, P * b : P * (b + 1)],
+                        weighted[(r, t)][:],
+                        ident[:],
+                        start=(r == 0),
+                        stop=(r == 1),
+                        is_transpose=True,
+                    )
+            total = keep.tile([P, w], F32, name=f"total{c}")
+            nc.scalar.copy(out=total[:], in_=back[:, 0:w])
+            nc.scalar.dma_start(out=out[:, P * u0[c] : P * u0[c] + w], in_=total[:])
+
+        for t, w in zip(starts(PLAIN_FETCHES), PLAIN_FETCHES):
+            fetch_plain(t, w)
+        turn(0)
+        for c in range(len(TURNED_UNITS)):
+            if c + 1 < len(TURNED_UNITS):
+                turn(c + 1)
+            weigh(c)
+            turn_back(c)
+
+        d0 = starts(DIRECT_CHUNKS)
+        terms = [keep.tile([P, 2, w], F32, name=f"terms{c}") for c, w in enumerate(DIRECT_CHUNKS)]
+
+        def fetch_weighted(c, r):
+            w = DIRECT_CHUNKS[c]
+            t = turned_tokens + d0[c]
             nc.vector.tensor_tensor(
                 terms[c][:, r, :],
-                y[:].indirect(lst[:, t0[c] // 16 : (t0[c] + w) // 16]),
-                gates[:, r, t0[c] : t0[c] + w],
+                y[:].indirect(lists[r][:, t // 16 : (t + w) // 16]),
+                gates[:, r, d0[c] : d0[c] + w],
                 MULT,
             )
 
-        def finish(c):
-            w = TOKEN_CHUNKS[c]
-            if c < TENSOR_ADDS:
-                turned = bank(4 + c)
-                for a in range(0, w, P):
-                    for r in range(2):
-                        nc.tensor.matmul(
-                            turned[:, a : a + P],
-                            terms[c][:, r, a : a + P],
-                            ident[:],
-                            start=(r == 0),
-                            stop=(r == 1),
-                            is_transpose=True,
-                        )
-                by_token = keep.tile([P, w], F32, name=f"by_token{c}")
-                nc.scalar.copy(out=by_token[:], in_=turned[:, 0:w])
-                back = bank(6 + c)
-                for a in range(0, w, P):
-                    nc.tensor.transpose(back[:, a : a + P], by_token[:, a : a + P], ident[:])
-                nc.scalar.copy(out=sums[c][:], in_=back[:, 0:w])
-            else:
-                nc.vector.tensor_tensor(sums[c][:], terms[c][:, 0, :], terms[c][:, 1, :], ADD)
-            queue = nc.scalar if c < TENSOR_ADDS else nc.sync
-            queue.dma_start(out=out[:, t0[c] : t0[c] + w], in_=sums[c][:])
+        def add_terms(c):
+            w = DIRECT_CHUNKS[c]
+            t = turned_tokens + d0[c]
+            total = keep.tile([P, w], F32, name=f"direct_total{c}")
+            nc.vector.tensor_tensor(total[:], terms[c][:, 0, :], terms[c][:, 1, :], ADD)
+            nc.sync.dma_start(out=out[:, t : t + w], in_=total[:])
 
-        for c in range(ntok + 1):
-            if c < ntok:
-                fetch(c, 0)
+        for c in range(len(DIRECT_CHUNKS) + 1):
+            if c < len(DIRECT_CHUNKS):
+                fetch_weighted(c, 0)
             if c >= 1:
-                finish(c - 1)
-            if c < ntok:
-                fetch(c, 1)
+                add_terms(c - 1)
+            if c < len(DIRECT_CHUNKS):
+                fetch_weighted(c, 1)

@@ -15,7 +15,6 @@ U8 = mybir.dt.uint8
 FP8X4 = mybir.dt.float8_e4m3fn_x4
 FP4X4 = mybir.dt.float4_e2m1fn_x4
 SILU = mybir.ActivationFunctionType.Silu
-COPY = mybir.ActivationFunctionType.Copy
 MULT = mybir.AluOpType.mult
 ADD = mybir.AluOpType.add
 
@@ -23,13 +22,12 @@ P = 128
 PASSES = K // 512
 S = E * C
 HALF = T // 2
-SLOT_CHUNKS = [512, 512, 512, 256, 128, 128]
+SLOT_CHUNKS = [512, 512, 256, 256, 256, 128, 128]
 WARM_WIDTHS = [512, 512, 256]
 FIRST_GATHERS = [768, 768, 512]
 SECOND_GATHERS = [512, 512, 512, 256, 256]
-PLAIN_FETCHES = [256, 384]
-TURNED_UNITS = [2, 2, 1]
-DIRECT_CHUNKS = [256, 128]
+TOKEN_CHUNKS = [256, 256, 128, 256, 128]
+TENSOR_ADDS = 3
 
 
 def starts(widths):
@@ -67,7 +65,7 @@ def tile_moe_sup_lin_silu_kernel(
         for r in range(4):
             load_scale_rows(w1s_raw, w1_scales, r)
         x_lo = [keep.tile([P, HALF], I32, name=f"x_lo{s}", align_bytes=64) for s in range(PASSES)]
-        x_up = [keep.tile([P, PASSES, 256], I32, name=f"x_up{j}", align_bytes=64) for j in range(2)]
+        x_up = keep.tile([P, PASSES, HALF], I32, align_bytes=64)
         load_scale_rows(xs, x_scales, 0)
         load_scale_rows(xs, x_scales, 1)
         nc.sync.dma_start(out=x_lo[0][:], in_=xw[:, 0, 0:HALF])
@@ -76,7 +74,9 @@ def tile_moe_sup_lin_silu_kernel(
         for s in range(1, PASSES):
             nc.sync.dma_start(out=x_lo[s][:], in_=xw[:, s, 0:HALF])
         for j in range(2):
-            nc.sync.dma_start(out=x_up[j][:], in_=xw[:, :, HALF + 256 * j : HALF + 256 * (j + 1)])
+            nc.sync.dma_start(
+                out=x_up[:, :, 256 * j : 256 * (j + 1)], in_=xw[:, :, HALF + 256 * j : HALF + 256 * (j + 1)]
+            )
         slot_list = keep.tile([P, S // 16], U16)
         nc.sync.dma_start(slot_list[:], offs)
 
@@ -117,16 +117,8 @@ def tile_moe_sup_lin_silu_kernel(
         pos_b = keep.tile([P, T // 16], U16)
         nc.sync.dma_start(pos_a[:], pos1)
         nc.sync.dma_start(pos_b[:], pos2)
-        turned_tokens = sum(PLAIN_FETCHES)
-        blocks = T // P
-        gate_rows = keep.tile([P, P], F32)
-        nc.vector.memset(gate_rows[:], 0.0)
-        for r in range(2):
-            nc.sync.dma_start(
-                out=gate_rows[blocks * r : blocks * (r + 1), :], in_=gate[r, 0, :].rearrange("(b t) -> b t", t=P)
-            )
-        gates = keep.tile([P, 2, T - turned_tokens], F32)
-        nc.sync.dma_start(out=gates[:], in_=gate[:, :, turned_tokens:T].rearrange("r p t -> p r t"))
+        gates = keep.tile([P, 2, T], F32)
+        nc.sync.dma_start(out=gates[:], in_=gate.rearrange("r p t -> p r t"))
 
         ident = keep.tile([P, P], F32, name="ident", tag="w1s_raw", align_bytes=64)
         make_identity(nc, ident[:])
@@ -141,8 +133,7 @@ def tile_moe_sup_lin_silu_kernel(
                 if t0 < HALF:
                     rhs = x_lo[s][:, t0 : t0 + width]
                 else:
-                    j, a = divmod(t0 - HALF, 256)
-                    rhs = x_up[j][:, s, a : a + width]
+                    rhs = x_up[:, s, t0 - HALF : t0 - HALF + width]
                 nc.tensor.matmul_mx(
                     out=acc,
                     lhsT=w1w[u][:, e, s, :].bitcast(FP4X4),
@@ -169,20 +160,19 @@ def tile_moe_sup_lin_silu_kernel(
                 SILU,
             )
 
-        wide(0, 0, 0, 0)
-        wide(1, 0, 1, 0)
+        planes = keep.tile([P, 2, HALF], BF16, align_bytes=64)
+        for e in range(2):
+            acc = bank(e)
+            first_layer(acc[:], 0, e, 0, HALF)
+            nc.scalar.activation(planes[:, e, :], acc[:], SILU)
+        nc.vector.tensor_copy(out=h_view(0)[:, 0:HALF, :], in_=planes[:].rearrange("p e t -> p t e"))
         narrow(2, 0, HALF, 2)
         narrow(3, 0, HALF + 2 * P, 1)
         narrow(4, 0, HALF + 3 * P, 1)
+        wide(5, 1, 0, HALF)
+        wide(6, 1, 1, HALF)
         wide(3, 1, 0, 0)
         wide(4, 1, 1, 0)
-        narrow(3, 1, HALF, 2)
-        narrow(4, 1, HALF + 2 * P, 2)
-
-        gate_bank = bank(4)
-        nc.tensor.transpose(gate_bank[:, 0:P], gate_rows[:], ident[:])
-        gate_cols = keep.tile([P, 2 * blocks], F32)
-        nc.scalar.copy(out=gate_cols[:], in_=gate_bank[:, 0 : 2 * blocks])
 
         y = keep.tile([P, S], F32)
         pairs = keep.tile([P, 2, S], U32)
@@ -203,7 +193,7 @@ def tile_moe_sup_lin_silu_kernel(
             nc.vector.quantize_mx(
                 out=codes[:, a : a + w].bitcast(FP8X4), scales=scales[:, a : a + w], in_=grouped[:, 4 * a : 4 * (a + w)]
             )
-            acc = bank((2, 5, 6, 7)[c % 4])
+            acc = bank((0, 1, 2, 7, 5, 6, 3)[c])
             step = min(w, C)
             for j in range(0, w, step):
                 e = (a + j) // C
@@ -216,7 +206,7 @@ def tile_moe_sup_lin_silu_kernel(
                     start=True,
                     stop=True,
                 )
-            if a + w == S:
+            if c in (4, 6):
                 nc.vector.tensor_copy(out=y[:, a : a + w], in_=acc[:, 0:w])
             else:
                 nc.scalar.copy(out=y[:, a : a + w], in_=acc[:, 0:w])
@@ -230,88 +220,60 @@ def tile_moe_sup_lin_silu_kernel(
             second_layer(c, a, w)
 
         lists = (pos_a, pos_b)
-        fetched = {}
-        weighted = {}
-        u0 = starts(TURNED_UNITS)
+        t0 = starts(TOKEN_CHUNKS)
+        terms = [
+            [keep.tile([P, w], F32, name=f"term{c}_{r}") for r in range(2)] for c, w in enumerate(TOKEN_CHUNKS)
+        ]
         turned = {}
 
-        def fetch_plain(t, w):
-            for r in range(2):
-                got = keep.tile([P, w], F32, name=f"fetched{t}_{r}")
-                nc.vector.tensor_copy(got[:], y[:].indirect(lists[r][:, t // 16 : (t + w) // 16]))
-                for a in range(0, w, P):
-                    fetched[(r, t + a)] = got[:, a : a + P]
+        def fetch(c, r):
+            t, w = t0[c], TOKEN_CHUNKS[c]
+            nc.vector.tensor_tensor(
+                terms[c][r][:], y[:].indirect(lists[r][:, t // 16 : (t + w) // 16]), gates[:, r, t : t + w], MULT
+            )
 
-        def turn(c):
+        def turn_and_add(c):
             turned[c] = bank(c % 2)
-            for r in range(2):
-                for b in range(TURNED_UNITS[c]):
-                    col = P * (2 * r + b)
-                    t = P * (u0[c] + b)
-                    nc.tensor.transpose(turned[c][:, col : col + P], fetched[(r, t)], ident[:])
-
-        def weigh(c):
-            for r in range(2):
-                for b in range(TURNED_UNITS[c]):
-                    col = P * (2 * r + b)
-                    t = P * (u0[c] + b)
-                    g = blocks * r + u0[c] + b
-                    weighted[(r, t)] = keep.tile([P, P], F32, name=f"weighted{t}_{r}")
-                    nc.scalar.activation(
-                        weighted[(r, t)][:], turned[c][:, col : col + P], COPY, scale=gate_cols[:, g : g + 1]
-                    )
-
-        def turn_back(c):
-            back = bank(3 + c % 2)
-            w = P * TURNED_UNITS[c]
-            for b in range(TURNED_UNITS[c]):
-                t = P * (u0[c] + b)
+            for a in range(0, TOKEN_CHUNKS[c], P):
                 for r in range(2):
                     nc.tensor.matmul(
-                        back[:, P * b : P * (b + 1)],
-                        weighted[(r, t)][:],
+                        turned[c][:, a : a + P],
+                        terms[c][r][:, a : a + P],
                         ident[:],
                         start=(r == 0),
                         stop=(r == 1),
                         is_transpose=True,
                     )
+
+        def turn_back(c):
+            t, w = t0[c], TOKEN_CHUNKS[c]
+            by_token = keep.tile([P, w], F32, name=f"by_token{c}")
+            nc.scalar.copy(out=by_token[:], in_=turned[c][:, 0:w])
+            back = bank(4 + c)
+            for a in range(0, w, P):
+                nc.tensor.transpose(back[:, a : a + P], by_token[:, a : a + P], ident[:])
             total = keep.tile([P, w], F32, name=f"total{c}")
             nc.scalar.copy(out=total[:], in_=back[:, 0:w])
-            nc.scalar.dma_start(out=out[:, P * u0[c] : P * u0[c] + w], in_=total[:])
-
-        for t, w in zip(starts(PLAIN_FETCHES), PLAIN_FETCHES):
-            fetch_plain(t, w)
-        turn(0)
-        for c in range(len(TURNED_UNITS)):
-            if c + 1 < len(TURNED_UNITS):
-                turn(c + 1)
-            weigh(c)
-            turn_back(c)
-
-        d0 = starts(DIRECT_CHUNKS)
-        terms = [keep.tile([P, 2, w], F32, name=f"terms{c}") for c, w in enumerate(DIRECT_CHUNKS)]
-
-        def fetch_weighted(c, r):
-            w = DIRECT_CHUNKS[c]
-            t = turned_tokens + d0[c]
-            nc.vector.tensor_tensor(
-                terms[c][:, r, :],
-                y[:].indirect(lists[r][:, t // 16 : (t + w) // 16]),
-                gates[:, r, d0[c] : d0[c] + w],
-                MULT,
-            )
+            nc.scalar.dma_start(out=out[:, t : t + w], in_=total[:])
 
         def add_terms(c):
-            w = DIRECT_CHUNKS[c]
-            t = turned_tokens + d0[c]
-            total = keep.tile([P, w], F32, name=f"direct_total{c}")
-            nc.vector.tensor_tensor(total[:], terms[c][:, 0, :], terms[c][:, 1, :], ADD)
+            t, w = t0[c], TOKEN_CHUNKS[c]
+            total = keep.tile([P, w], F32, name=f"total{c}")
+            nc.vector.tensor_tensor(total[:], terms[c][0][:], terms[c][1][:], ADD)
             nc.sync.dma_start(out=out[:, t : t + w], in_=total[:])
 
-        for c in range(len(DIRECT_CHUNKS) + 1):
-            if c < len(DIRECT_CHUNKS):
-                fetch_weighted(c, 0)
-            if c >= 1:
+        for c in range(TENSOR_ADDS):
+            fetch(c, 0)
+            fetch(c, 1)
+        turn_and_add(0)
+        for c in range(TENSOR_ADDS):
+            if c + 1 < TENSOR_ADDS:
+                turn_and_add(c + 1)
+            turn_back(c)
+        for c in range(TENSOR_ADDS, len(TOKEN_CHUNKS) + 1):
+            if c < len(TOKEN_CHUNKS):
+                fetch(c, 0)
+            if c > TENSOR_ADDS:
                 add_terms(c - 1)
-            if c < len(DIRECT_CHUNKS):
-                fetch_weighted(c, 1)
+            if c < len(TOKEN_CHUNKS):
+                fetch(c, 1)

@@ -23,9 +23,9 @@ PASSES = K // 512
 S = E * C
 HALF = T // 2
 SLOT_CHUNKS = [512, 512, 256, 256, 256, 128, 128]
+UPPER_PIECES = [256, 128, 128]
 WARM_WIDTHS = [512, 512, 256]
-FIRST_GATHERS = [768, 768, 512]
-SECOND_GATHERS = [512, 512, 512, 256, 256]
+EDGE = 256
 TOKEN_CHUNKS = [256, 256, 128, 256, 128]
 TENSOR_ADDS = 3
 
@@ -66,17 +66,12 @@ def tile_moe_sup_lin_silu_kernel(
             load_scale_rows(w1s_raw, w1_scales, r)
         x_lo = [keep.tile([P, HALF], I32, name=f"x_lo{s}", align_bytes=64) for s in range(PASSES)]
         x_up = keep.tile([P, PASSES, HALF], I32, align_bytes=64)
-        load_scale_rows(xs, x_scales, 0)
-        load_scale_rows(xs, x_scales, 1)
-        nc.sync.dma_start(out=x_lo[0][:], in_=xw[:, 0, 0:HALF])
-        load_scale_rows(xs, x_scales, 2)
-        load_scale_rows(xs, x_scales, 3)
-        for s in range(1, PASSES):
+        for r in range(4):
+            load_scale_rows(xs, x_scales, r)
+        for s in range(PASSES):
             nc.sync.dma_start(out=x_lo[s][:], in_=xw[:, s, 0:HALF])
-        for j in range(2):
-            nc.sync.dma_start(
-                out=x_up[:, :, 256 * j : 256 * (j + 1)], in_=xw[:, :, HALF + 256 * j : HALF + 256 * (j + 1)]
-            )
+        for a, w in zip(starts(UPPER_PIECES), UPPER_PIECES):
+            nc.sync.dma_start(out=x_up[:, :, a : a + w], in_=xw[:, :, HALF + a : HALF + a + w])
         slot_list = keep.tile([P, S // 16], U16)
         nc.sync.dma_start(slot_list[:], offs)
 
@@ -175,18 +170,19 @@ def tile_moe_sup_lin_silu_kernel(
         wide(4, 1, 1, 0)
 
         y = keep.tile([P, S], F32)
-        pairs = keep.tile([P, 2, S], U32)
         grouped = keep.tile([P, 4 * S], BF16, align_bytes=64)
         codes = keep.tile([P, S], U32, align_bytes=64)
         scales = keep.tile([P, S], U8, align_bytes=64)
 
-        def gather(u, a, w):
-            nc.vector.tensor_copy(pairs[:, u, a : a + w], h[u][:].indirect(slot_list[:, a // 16 : (a + w) // 16]))
+        def gather(pairs, base, u, a, w):
+            nc.vector.tensor_copy(
+                pairs[:, u, a - base : a - base + w], h[u][:].indirect(slot_list[:, a // 16 : (a + w) // 16])
+            )
 
-        def interleave(a, w):
+        def interleave(pairs, base, a, w):
             nc.scalar.copy(
-                out=grouped[:, 4 * a : 4 * (a + w)].bitcast(U32).rearrange("p (n u) -> p n u", u=2),
-                in_=pairs[:, :, a : a + w].rearrange("p u n -> p n u"),
+                out=grouped[:, 4 * a : 4 * (a + w)].bitcast(F32).rearrange("p (n u) -> p n u", u=2),
+                in_=pairs[:, :, a - base : a - base + w].bitcast(F32).rearrange("p u n -> p n u"),
             )
 
         def second_layer(c, a, w):
@@ -211,11 +207,20 @@ def tile_moe_sup_lin_silu_kernel(
             else:
                 nc.scalar.copy(out=y[:, a : a + w], in_=acc[:, 0:w])
 
-        for a, w in zip(starts(FIRST_GATHERS), FIRST_GATHERS):
-            gather(0, a, w)
-        for a, w in zip(starts(SECOND_GATHERS), SECOND_GATHERS):
-            gather(1, a, w)
-            interleave(a, w)
+        edge = keep.tile([P, 2, EDGE], U32, name="first_pairs", tag="edge")
+        middle = keep.tile([P, 2, S - 2 * EDGE], U32)
+        gather(edge, 0, 0, 0, EDGE)
+        for a in range(EDGE, S - EDGE, 768):
+            gather(middle, EDGE, 0, a, 768)
+        gather(edge, 0, 1, 0, EDGE)
+        interleave(edge, 0, 0, EDGE)
+        for a in range(EDGE, S - EDGE, 512):
+            gather(middle, EDGE, 1, a, 512)
+            interleave(middle, EDGE, a, 512)
+        edge = keep.tile([P, 2, EDGE], U32, name="last_pairs", tag="edge")
+        for u in range(2):
+            gather(edge, S - EDGE, u, S - EDGE, EDGE)
+        interleave(edge, S - EDGE, S - EDGE, EDGE)
         for c, (a, w) in enumerate(zip(starts(SLOT_CHUNKS), SLOT_CHUNKS)):
             second_layer(c, a, w)
 

@@ -45,7 +45,8 @@ def tile_moe_sup_lin_silu_kernel(
         def bank(b):
             return psum.tile([P, 512], F32, name=f"bank{b}", tag=f"bank{b}")
 
-        w1w_raw = keep.tile([P, PASSES, 2 * H], U8, align_bytes=64)
+        w1w_first = keep.tile([P, 1, 2 * H], U8, align_bytes=64)
+        w1w_rest = keep.tile([P, PASSES - 1, 2 * H], U8, align_bytes=64)
         w1s_raw = keep.tile([P, PASSES, H], U8, tag="w1s_raw", align_bytes=64)
         xs = keep.tile([P, PASSES, T], U8, align_bytes=64)
         w2w = keep.tile([P, E, 2 * N], U8, align_bytes=64)
@@ -55,7 +56,8 @@ def tile_moe_sup_lin_silu_kernel(
         nc.vector.memset(w1s_raw[:].bitcast(I32), 0)
         nc.vector.memset(xs[:].bitcast(I32), 0)
 
-        nc.sync.dma_start(out=w1w_raw[:].bitcast(I32), in_=w1_words.rearrange("s p n -> p s n").bitcast(I32))
+        w1_rows = w1_words.rearrange("s p n -> p s n").bitcast(I32)
+        nc.sync.dma_start(out=w1w_first[:].bitcast(I32), in_=w1_rows[:, 0:1, :])
 
         def load_scale_rows(plane, source, r):
             nc.sync.dma_start(
@@ -68,7 +70,9 @@ def tile_moe_sup_lin_silu_kernel(
         x_up = keep.tile([P, PASSES, HALF], I32, align_bytes=64)
         for r in range(4):
             load_scale_rows(xs, x_scales, r)
-        for s in range(PASSES):
+        nc.sync.dma_start(out=x_lo[0][:], in_=xw[:, 0, 0:HALF])
+        nc.sync.dma_start(out=w1w_rest[:].bitcast(I32), in_=w1_rows[:, 1:PASSES, :])
+        for s in range(1, PASSES):
             nc.sync.dma_start(out=x_lo[s][:], in_=xw[:, s, 0:HALF])
         for a, w in zip(starts(UPPER_PIECES), UPPER_PIECES):
             nc.sync.dma_start(out=x_up[:, :, a : a + w], in_=xw[:, :, HALF + a : HALF + a + w])
@@ -81,28 +85,33 @@ def tile_moe_sup_lin_silu_kernel(
         nc.vector.memset(zeros[:], 0.0)
         nc.vector.quantize_mx(out=zero_codes[:].bitcast(FP8X4), scales=zero_scales[:], in_=zeros[:])
         scratch = bank(7)
-        for s, w in enumerate(WARM_WIDTHS):
+        for w in WARM_WIDTHS:
             nc.tensor.matmul_mx(
                 out=scratch[:, 0:w],
                 lhsT=zero_codes[:].bitcast(FP8X4),
                 lhsT_scale=zero_scales[:],
-                rhs=w1w_raw[:, s, 0 : 2 * w].bitcast(FP4X4),
-                rhs_scale=w1s_raw[:, s, 0:w],
+                rhs=w1w_first[:, 0, 0 : 2 * w].bitcast(FP4X4),
+                rhs_scale=w1s_raw[:, 0, 0:w],
                 start=True,
                 stop=True,
             )
 
         w1w = [keep.tile([P, 2, PASSES, 2 * P], U8, name=f"w1w{u}", align_bytes=64) for u in range(2)]
         w1s = [keep.tile([P, 2, PASSES, P], U8, name=f"w1s{u}", align_bytes=64) for u in range(2)]
-        for u in range(2):
+
+        def regroup_words(u, raw, first, count):
             nc.vector.tensor_copy(
-                out=w1w[u][:].bitcast(U16),
-                in_=w1w_raw[:].bitcast(U16).rearrange("p s (m t) -> p t s m", t=4)[:, 2 * u : 2 * u + 2],
+                out=w1w[u][:, :, first : first + count, :].bitcast(U16),
+                in_=raw[:].bitcast(U16).rearrange("p s (m t) -> p t s m", t=4)[:, 2 * u : 2 * u + 2],
             )
+
+        for u in range(2):
+            regroup_words(u, w1w_first, 0, 1)
             nc.vector.tensor_copy(
                 out=w1s[u][:],
                 in_=w1s_raw[:].rearrange("p s (m t) -> p t s m", t=4)[:, 2 * u : 2 * u + 2],
             )
+            regroup_words(u, w1w_rest, 1, PASSES - 1)
 
         nc.vector.memset(w2s[:].bitcast(I32), 0)
         nc.sync.dma_start(out=w2w[:].bitcast(I32), in_=w2_words.rearrange("e g p n -> p (e g) n").bitcast(I32))
@@ -156,11 +165,15 @@ def tile_moe_sup_lin_silu_kernel(
             )
 
         planes = keep.tile([P, 2, HALF], BF16, align_bytes=64)
+        accs = [bank(e) for e in range(2)]
         for e in range(2):
-            acc = bank(e)
-            first_layer(acc[:], 0, e, 0, HALF)
-            nc.scalar.activation(planes[:, e, :], acc[:], SILU)
-        nc.vector.tensor_copy(out=h_view(0)[:, 0:HALF, :], in_=planes[:].rearrange("p e t -> p t e"))
+            first_layer(accs[e][:], 0, e, 0, HALF)
+        nc.scalar.activation(planes[:, 0, :], accs[0][:], SILU)
+        for a in range(0, HALF, 256):
+            nc.scalar.activation(planes[:, 1, a : a + 256], accs[1][:, a : a + 256], SILU)
+            nc.vector.tensor_copy(
+                out=h_view(0)[:, a : a + 256, :], in_=planes[:, :, a : a + 256].rearrange("p e t -> p t e")
+            )
         narrow(2, 0, HALF, 2)
         narrow(3, 0, HALF + 2 * P, 1)
         narrow(4, 0, HALF + 3 * P, 1)
@@ -214,9 +227,9 @@ def tile_moe_sup_lin_silu_kernel(
             gather(middle, EDGE, 0, a, 768)
         gather(edge, 0, 1, 0, EDGE)
         interleave(edge, 0, 0, EDGE)
-        for a in range(EDGE, S - EDGE, 512):
-            gather(middle, EDGE, 1, a, 512)
-            interleave(middle, EDGE, a, 512)
+        for a in range(EDGE, S - EDGE, 768):
+            gather(middle, EDGE, 1, a, 768)
+            interleave(middle, EDGE, a, 768)
         edge = keep.tile([P, 2, EDGE], U32, name="last_pairs", tag="edge")
         for u in range(2):
             gather(edge, S - EDGE, u, S - EDGE, EDGE)

@@ -24,7 +24,6 @@ S = E * C
 HALF = T // 2
 SLOT_CHUNKS = [512, 512, 256, 256, 256, 128, 128]
 UPPER_PIECES = [256, 128, 128]
-WARM_WIDTHS = [512, 512, 256]
 EDGE = 256
 TOKEN_CHUNKS = [256, 256, 128, 256, 128]
 TENSOR_ADDS = 3
@@ -46,8 +45,8 @@ def tile_moe_sup_lin_silu_kernel(
             return psum.tile([P, 512], F32, name=f"bank{b}", tag=f"bank{b}")
 
         w1w_first = keep.tile([P, 1, 2 * H], U8, align_bytes=64)
-        w1w_rest = keep.tile([P, PASSES - 1, 2 * H], U8, align_bytes=64)
-        w1s_raw = keep.tile([P, PASSES, H], U8, tag="w1s_raw", align_bytes=64)
+        w1w_rest = keep.tile([P, PASSES - 1, 2 * H], U8, tag="w1w_rest", align_bytes=64)
+        w1s_raw = keep.tile([P, PASSES, H], U8, align_bytes=64)
         xs = keep.tile([P, PASSES, T], U8, align_bytes=64)
         w2w = keep.tile([P, E, 2 * N], U8, align_bytes=64)
         w2s = keep.tile([P, E, N], U8, align_bytes=64)
@@ -79,23 +78,6 @@ def tile_moe_sup_lin_silu_kernel(
         slot_list = keep.tile([P, S // 16], U16)
         nc.sync.dma_start(slot_list[:], offs)
 
-        zeros = keep.tile([P, 4 * P], BF16, align_bytes=64)
-        zero_codes = keep.tile([P, P], U32, align_bytes=64)
-        zero_scales = keep.tile([P, P], U8, align_bytes=64)
-        nc.vector.memset(zeros[:], 0.0)
-        nc.vector.quantize_mx(out=zero_codes[:].bitcast(FP8X4), scales=zero_scales[:], in_=zeros[:])
-        scratch = bank(7)
-        for w in WARM_WIDTHS:
-            nc.tensor.matmul_mx(
-                out=scratch[:, 0:w],
-                lhsT=zero_codes[:].bitcast(FP8X4),
-                lhsT_scale=zero_scales[:],
-                rhs=w1w_first[:, 0, 0 : 2 * w].bitcast(FP4X4),
-                rhs_scale=w1s_raw[:, 0, 0:w],
-                start=True,
-                stop=True,
-            )
-
         w1w = [keep.tile([P, 2, PASSES, 2 * P], U8, name=f"w1w{u}", align_bytes=64) for u in range(2)]
         w1s = [keep.tile([P, 2, PASSES, P], U8, name=f"w1s{u}", align_bytes=64) for u in range(2)]
 
@@ -124,7 +106,7 @@ def tile_moe_sup_lin_silu_kernel(
         gates = keep.tile([P, 2, T], F32)
         nc.sync.dma_start(out=gates[:], in_=gate.rearrange("r p t -> p r t"))
 
-        ident = keep.tile([P, P], F32, name="ident", tag="w1s_raw", align_bytes=64)
+        ident = keep.tile([P, P], F32, name="ident", tag="w1w_rest", align_bytes=64)
         make_identity(nc, ident[:])
 
         h = [keep.tile([P, T], U32, name=f"h{u}", align_bytes=64) for u in range(2)]

@@ -14,6 +14,7 @@ U16 = mybir.dt.uint16
 U8 = mybir.dt.uint8
 FP8X4 = mybir.dt.float8_e4m3fn_x4
 FP4X4 = mybir.dt.float4_e2m1fn_x4
+COPY = mybir.ActivationFunctionType.Copy
 SILU = mybir.ActivationFunctionType.Silu
 MULT = mybir.AluOpType.mult
 ADD = mybir.AluOpType.add
@@ -24,7 +25,10 @@ S = E * C
 HALF = T // 2
 SLOT_CHUNKS = [512, 512, 256, 256, 256, 128, 128]
 UPPER_PIECES = [256, 128, 128]
-EDGE = 256
+FRONT = 128
+BACK = 256
+FIRST_GATHERS = [768, 768, 128]
+SECOND_GATHERS = [384, 768, 512]
 TOKEN_CHUNKS = [256, 256, 128, 256, 128]
 TENSOR_ADDS = 3
 
@@ -145,24 +149,35 @@ def tile_moe_sup_lin_silu_kernel(
                 acc[:, 0 : 2 * P * groups].rearrange("p (j e t) -> p j t e", e=2, t=P),
                 SILU,
             )
+            return acc
 
-        planes = keep.tile([P, 2, HALF], BF16, align_bytes=64)
+        planes = keep.tile([P, 2, T], BF16, align_bytes=64)
         accs = [bank(e) for e in range(2)]
         for e in range(2):
             first_layer(accs[e][:], 0, e, 0, HALF)
-        nc.scalar.activation(planes[:, 0, :], accs[0][:], SILU)
+        nc.scalar.activation(planes[:, 0, 0:HALF], accs[0][:], SILU)
         for a in range(0, HALF, 256):
             nc.scalar.activation(planes[:, 1, a : a + 256], accs[1][:, a : a + 256], SILU)
             nc.vector.tensor_copy(
                 out=h_view(0)[:, a : a + 256, :], in_=planes[:, :, a : a + 256].rearrange("p e t -> p t e")
             )
+
+        def part(t0, w):
+            nc.vector.tensor_copy(
+                out=planes[:, :, t0 : t0 + w], in_=h_view(0)[:, t0 : t0 + w, :].rearrange("p t e -> p e t")
+            )
+
         narrow(2, 0, HALF, 2)
+        part(HALF, 2 * P)
         narrow(3, 0, HALF + 2 * P, 1)
-        narrow(4, 0, HALF + 3 * P, 1)
+        part(HALF + 2 * P, P)
+        last = narrow(4, 0, HALF + 3 * P, 1)
+        nc.scalar.activation(planes[:, :, T - P : T], last[:, 0 : 2 * P].rearrange("p (e t) -> p e t", e=2), SILU)
         wide(5, 1, 0, HALF)
         wide(6, 1, 1, HALF)
-        wide(3, 1, 0, 0)
-        wide(4, 1, 1, 0)
+        narrow(3, 1, 0, 2)
+        narrow(4, 1, 2 * P, 1)
+        narrow(5, 1, 3 * P, 1)
 
         y = keep.tile([P, S], F32)
         grouped = keep.tile([P, 4 * S], BF16, align_bytes=64)
@@ -202,20 +217,28 @@ def tile_moe_sup_lin_silu_kernel(
             else:
                 nc.scalar.copy(out=y[:, a : a + w], in_=acc[:, 0:w])
 
-        edge = keep.tile([P, 2, EDGE], U32, name="first_pairs", tag="edge")
-        middle = keep.tile([P, 2, S - 2 * EDGE], U32)
-        gather(edge, 0, 0, 0, EDGE)
-        for a in range(EDGE, S - EDGE, 768):
-            gather(middle, EDGE, 0, a, 768)
-        gather(edge, 0, 1, 0, EDGE)
-        interleave(edge, 0, 0, EDGE)
-        for a in range(EDGE, S - EDGE, 768):
-            gather(middle, EDGE, 1, a, 768)
-            interleave(middle, EDGE, a, 768)
-        edge = keep.tile([P, 2, EDGE], U32, name="last_pairs", tag="edge")
-        for u in range(2):
-            gather(edge, S - EDGE, u, S - EDGE, EDGE)
-        interleave(edge, S - EDGE, S - EDGE, EDGE)
+        def gather_rows(pairs, a, w):
+            for e in range(2):
+                nc.scalar.activation(
+                    pairs[:, 0, :].bitcast(BF16).rearrange("p (n e) -> p n e", e=2)[:, :, e],
+                    planes[:, e, :].indirect(slot_list[:, a // 16 : (a + w) // 16]),
+                    COPY,
+                )
+
+        front = keep.tile([P, 2, FRONT], U32)
+        rest = keep.tile([P, 2, S - FRONT - BACK], U32)
+        back = keep.tile([P, 2, BACK], U32, name="back", tag="x_lo2", align_bytes=64)
+        gather_rows(front, 0, FRONT)
+        for a, w in zip(starts(FIRST_GATHERS), FIRST_GATHERS):
+            gather(rest, FRONT, 0, FRONT + a, w)
+        gather(front, 0, 1, 0, FRONT)
+        interleave(front, 0, 0, FRONT)
+        for a, w in zip(starts(SECOND_GATHERS), SECOND_GATHERS):
+            gather(rest, FRONT, 1, FRONT + a, w)
+            interleave(rest, FRONT, FRONT + a, w)
+        gather_rows(back, S - BACK, BACK)
+        gather(back, S - BACK, 1, S - BACK, BACK)
+        interleave(back, S - BACK, S - BACK, BACK)
         for c, (a, w) in enumerate(zip(starts(SLOT_CHUNKS), SLOT_CHUNKS)):
             second_layer(c, a, w)
 

@@ -23,14 +23,17 @@ P = 128
 PASSES = K // 512
 S = E * C
 HALF = T // 2
-SLOT_CHUNKS = [512, 512, 256, 256, 256, 128, 128]
+SLOT_CHUNKS = [(0, 512), (512, 256), (768, 512), (1280, 256), (1536, 256), (1792, 128), (1920, 128)]
 UPPER_PIECES = [256, 128, 128]
-FRONT = 128
-BACK = 256
-FIRST_GATHERS = [768, 768, 128]
-SECOND_GATHERS = [384, 768, 512]
-TOKEN_CHUNKS = [256, 256, 128, 256, 128]
-TENSOR_ADDS = 3
+BACK = 640
+FIRST_GATHERS = [768, 640]
+WOVEN_START = 0
+WOVEN_PIECES = [512, 256]
+SECOND_GATHERS = [384, 256]
+BACK_GATHERS = [384, 256]
+SCALAR_COPIES = 4
+TURNED_UNITS = [128, 128, 128]
+ADDED_UNITS = [384, 128, 128]
 
 
 def starts(widths):
@@ -151,7 +154,7 @@ def tile_moe_sup_lin_silu_kernel(
             )
             return acc
 
-        planes = keep.tile([P, 2, T], BF16, align_bytes=64)
+        planes = keep.tile([P, 2, T], BF16, tag="planes", align_bytes=64)
         accs = [bank(e) for e in range(2)]
         for e in range(2):
             first_layer(accs[e][:], 0, e, 0, HALF)
@@ -180,7 +183,6 @@ def tile_moe_sup_lin_silu_kernel(
         narrow(5, 1, 3 * P, 1)
 
         y = keep.tile([P, S], F32)
-        grouped = keep.tile([P, 4 * S], BF16, align_bytes=64)
         codes = keep.tile([P, S], U32, align_bytes=64)
         scales = keep.tile([P, S], U8, align_bytes=64)
 
@@ -196,9 +198,11 @@ def tile_moe_sup_lin_silu_kernel(
             )
 
         def second_layer(c, a, w):
-            nc.vector.quantize_mx(
-                out=codes[:, a : a + w].bitcast(FP8X4), scales=scales[:, a : a + w], in_=grouped[:, 4 * a : 4 * (a + w)]
-            )
+            if a < sum(WOVEN_PIECES):
+                values = woven[:, 2 * (a - WOVEN_START) : 2 * (a - WOVEN_START + w)].bitcast(BF16)
+            else:
+                values = grouped[:, 4 * a : 4 * (a + w)]
+            nc.vector.quantize_mx(out=codes[:, a : a + w].bitcast(FP8X4), scales=scales[:, a : a + w], in_=values)
             acc = bank((0, 1, 2, 7, 5, 6, 3)[c])
             step = min(w, C)
             for j in range(0, w, step):
@@ -212,10 +216,7 @@ def tile_moe_sup_lin_silu_kernel(
                     start=True,
                     stop=True,
                 )
-            if c in (4, 6):
-                nc.vector.tensor_copy(out=y[:, a : a + w], in_=acc[:, 0:w])
-            else:
-                nc.scalar.copy(out=y[:, a : a + w], in_=acc[:, 0:w])
+            return acc
 
         def gather_rows(pairs, a, w):
             for e in range(2):
@@ -225,78 +226,94 @@ def tile_moe_sup_lin_silu_kernel(
                     COPY,
                 )
 
-        front = keep.tile([P, 2, FRONT], U32)
-        rest = keep.tile([P, 2, S - FRONT - BACK], U32)
+        rest = keep.tile([P, 2, S - BACK], U32)
         back = keep.tile([P, 2, BACK], U32, name="back", tag="x_lo2", align_bytes=64)
-        gather_rows(front, 0, FRONT)
         for a, w in zip(starts(FIRST_GATHERS), FIRST_GATHERS):
-            gather(rest, FRONT, 0, FRONT + a, w)
-        gather(front, 0, 1, 0, FRONT)
-        interleave(front, 0, 0, FRONT)
-        for a, w in zip(starts(SECOND_GATHERS), SECOND_GATHERS):
-            gather(rest, FRONT, 1, FRONT + a, w)
-            interleave(rest, FRONT, FRONT + a, w)
+            gather(rest, 0, 0, a, w)
         gather_rows(back, S - BACK, BACK)
-        gather(back, S - BACK, 1, S - BACK, BACK)
-        interleave(back, S - BACK, S - BACK, BACK)
-        for c, (a, w) in enumerate(zip(starts(SLOT_CHUNKS), SLOT_CHUNKS)):
-            second_layer(c, a, w)
+        grouped = keep.tile([P, 4 * S], BF16, name="grouped", tag="planes", align_bytes=64)
+        woven = keep.tile([P, 2 * sum(WOVEN_PIECES)], U32, align_bytes=64)
+        gather(rest, 0, 1, WOVEN_START, sum(WOVEN_PIECES))
+        for a, w in zip(starts(WOVEN_PIECES), WOVEN_PIECES):
+            nc.gpsimd.tensor_copy(
+                out=woven[:, 2 * a : 2 * (a + w)].rearrange("p (n u) -> p n u", u=2),
+                in_=rest[:, :, WOVEN_START + a : WOVEN_START + a + w].rearrange("p u n -> p n u"),
+            )
+        for a, w in zip(starts(SECOND_GATHERS), SECOND_GATHERS):
+            gather(rest, 0, 1, sum(WOVEN_PIECES) + a, w)
+            interleave(rest, 0, sum(WOVEN_PIECES) + a, w)
+        for a, w in zip(starts(BACK_GATHERS), BACK_GATHERS):
+            gather(back, S - BACK, 1, S - BACK + a, w)
+            interleave(back, S - BACK, S - BACK + a, w)
+        chunks = SLOT_CHUNKS
+        sums = [second_layer(c, a, w) for c, (a, w) in enumerate(chunks)]
+        for c, (a, w) in enumerate(chunks):
+            if c < SCALAR_COPIES:
+                nc.scalar.copy(out=y[:, a : a + w], in_=sums[c][:, 0:w])
+            else:
+                nc.vector.tensor_copy(out=y[:, a : a + w], in_=sums[c][:, 0:w])
 
-        lists = (pos_a, pos_b)
-        t0 = starts(TOKEN_CHUNKS)
-        terms = [
-            [keep.tile([P, w], F32, name=f"term{c}_{r}") for r in range(2)] for c, w in enumerate(TOKEN_CHUNKS)
-        ]
+        first_terms = {}
+        second_terms = {}
+
+        def fetch(terms, r, t, w):
+            term = keep.tile([P, w], F32, name=f"term{r}_{t}")
+            nc.vector.tensor_tensor(
+                term[:], y[:].indirect((pos_a, pos_b)[r][:, t // 16 : (t + w) // 16]), gates[:, r, t : t + w], MULT
+            )
+            for a in range(0, w, P):
+                terms[t + a] = (term, a)
+
+        def piece(terms, t, w):
+            term, a = terms[t]
+            return term[:, a : a + w]
+
         turned = {}
 
-        def fetch(c, r):
-            t, w = t0[c], TOKEN_CHUNKS[c]
-            nc.vector.tensor_tensor(
-                terms[c][r][:], y[:].indirect(lists[r][:, t // 16 : (t + w) // 16]), gates[:, r, t : t + w], MULT
-            )
-
-        def turn_and_add(c):
+        def turn_and_add(c, t, w):
             turned[c] = bank(c % 2)
-            for a in range(0, TOKEN_CHUNKS[c], P):
-                for r in range(2):
+            for a in range(0, w, P):
+                for r, terms in enumerate((first_terms, second_terms)):
                     nc.tensor.matmul(
                         turned[c][:, a : a + P],
-                        terms[c][r][:, a : a + P],
+                        piece(terms, t + a, P),
                         ident[:],
                         start=(r == 0),
                         stop=(r == 1),
                         is_transpose=True,
                     )
 
-        def turn_back(c):
-            t, w = t0[c], TOKEN_CHUNKS[c]
+        def turn_back(c, t, w):
             by_token = keep.tile([P, w], F32, name=f"by_token{c}")
             nc.scalar.copy(out=by_token[:], in_=turned[c][:, 0:w])
             back = bank(4 + c)
             for a in range(0, w, P):
                 nc.tensor.transpose(back[:, a : a + P], by_token[:, a : a + P], ident[:])
-            total = keep.tile([P, w], F32, name=f"total{c}")
+            total = keep.tile([P, w], F32, name=f"total{t}")
             nc.scalar.copy(out=total[:], in_=back[:, 0:w])
             nc.scalar.dma_start(out=out[:, t : t + w], in_=total[:])
 
-        def add_terms(c):
-            t, w = t0[c], TOKEN_CHUNKS[c]
-            total = keep.tile([P, w], F32, name=f"total{c}")
-            nc.vector.tensor_tensor(total[:], terms[c][0][:], terms[c][1][:], ADD)
+        def add_terms(t, w):
+            total = keep.tile([P, w], F32, name=f"total{t}")
+            nc.vector.tensor_tensor(total[:], piece(first_terms, t, w), piece(second_terms, t, w), ADD)
             nc.sync.dma_start(out=out[:, t : t + w], in_=total[:])
 
-        for c in range(TENSOR_ADDS):
-            fetch(c, 0)
-            fetch(c, 1)
-        turn_and_add(0)
-        for c in range(TENSOR_ADDS):
-            if c + 1 < TENSOR_ADDS:
-                turn_and_add(c + 1)
-            turn_back(c)
-        for c in range(TENSOR_ADDS, len(TOKEN_CHUNKS) + 1):
-            if c < len(TOKEN_CHUNKS):
-                fetch(c, 0)
-            if c > TENSOR_ADDS:
-                add_terms(c - 1)
-            if c < len(TOKEN_CHUNKS):
-                fetch(c, 1)
+        turned_tokens = sum(TURNED_UNITS)
+        units = list(zip(starts(TURNED_UNITS), TURNED_UNITS))
+        fetch(first_terms, 0, *units[0])
+        fetch(second_terms, 1, *units[0])
+        fetch(first_terms, 0, units[1][0], turned_tokens - units[1][0])
+        for t, w in units[1:]:
+            fetch(second_terms, 1, t, w)
+        fetch(first_terms, 0, turned_tokens, T - turned_tokens)
+        added = [(turned_tokens + t, w) for t, w in zip(starts(ADDED_UNITS), ADDED_UNITS)]
+        fetch(second_terms, 1, *added[0])
+        for c in range(1, len(added)):
+            fetch(second_terms, 1, *added[c])
+            add_terms(*added[c - 1])
+        add_terms(*added[-1])
+        turn_and_add(0, *units[0])
+        for c in range(len(units)):
+            if c + 1 < len(units):
+                turn_and_add(c + 1, *units[c + 1])
+            turn_back(c, *units[c])

@@ -23,15 +23,15 @@ P = 128
 PASSES = K // 512
 S = E * C
 HALF = T // 2
-SLOT_CHUNKS = [(0, 512), (512, 256), (768, 512), (1280, 256), (1536, 256), (1792, 128), (1920, 128)]
+SLOT_CHUNKS = [(0, 512), (512, 512), (1024, 256), (1280, 256), (1536, 256), (1792, 128), (1920, 128)]
 UPPER_PIECES = [256, 128, 128]
 BACK = 640
 FIRST_GATHERS = [768, 640]
 WOVEN_START = 0
-WOVEN_PIECES = [512, 256]
-SECOND_GATHERS = [384, 256]
+WOVEN_PIECES = [512, 512]
+SECOND_GATHERS = [384]
 BACK_GATHERS = [384, 256]
-SCALAR_COPIES = 4
+VECTOR_COPIES = (3, 4, 5)
 TURNED_UNITS = [128, 128, 128]
 ADDED_UNITS = [384, 128, 128]
 
@@ -174,8 +174,10 @@ def tile_moe_sup_lin_silu_kernel(
         part(HALF, 2 * P)
         narrow(3, 0, HALF + 2 * P, 1)
         part(HALF + 2 * P, P)
-        last = narrow(4, 0, HALF + 3 * P, 1)
-        nc.scalar.activation(planes[:, :, T - P : T], last[:, 0 : 2 * P].rearrange("p (e t) -> p e t", e=2), SILU)
+        narrow(4, 0, HALF + 3 * P, 1)
+        nc.gpsimd.tensor_copy(
+            out=planes[:, :, T - P : T], in_=h_view(0)[:, T - P : T, :].rearrange("p t e -> p e t")
+        )
         wide(5, 1, 0, HALF)
         wide(6, 1, 1, HALF)
         narrow(3, 1, 0, 2)
@@ -233,8 +235,8 @@ def tile_moe_sup_lin_silu_kernel(
         gather_rows(back, S - BACK, BACK)
         grouped = keep.tile([P, 4 * S], BF16, name="grouped", tag="planes", align_bytes=64)
         woven = keep.tile([P, 2 * sum(WOVEN_PIECES)], U32, align_bytes=64)
-        gather(rest, 0, 1, WOVEN_START, sum(WOVEN_PIECES))
         for a, w in zip(starts(WOVEN_PIECES), WOVEN_PIECES):
+            gather(rest, 0, 1, WOVEN_START + a, w)
             nc.gpsimd.tensor_copy(
                 out=woven[:, 2 * a : 2 * (a + w)].rearrange("p (n u) -> p n u", u=2),
                 in_=rest[:, :, WOVEN_START + a : WOVEN_START + a + w].rearrange("p u n -> p n u"),
@@ -248,7 +250,7 @@ def tile_moe_sup_lin_silu_kernel(
         chunks = SLOT_CHUNKS
         sums = [second_layer(c, a, w) for c, (a, w) in enumerate(chunks)]
         for c, (a, w) in enumerate(chunks):
-            if c < SCALAR_COPIES:
+            if c not in VECTOR_COPIES:
                 nc.scalar.copy(out=y[:, a : a + w], in_=sums[c][:, 0:w])
             else:
                 nc.vector.tensor_copy(out=y[:, a : a + w], in_=sums[c][:, 0:w])

@@ -1,7 +1,6 @@
 from contextlib import ExitStack
 
 import concourse.mybir as mybir
-from concourse.masks import make_identity
 
 K, T, E, C, H, N = 1536, 1024, 8, 256, 512, 128
 FLOPS = 2 * K * H * T + 2 * H * N * E * C
@@ -32,8 +31,7 @@ WOVEN_PIECES = [512, 512]
 SECOND_GATHERS = [384]
 BACK_GATHERS = [384, 256]
 VECTOR_COPIES = (3, 4, 5)
-TURNED_UNITS = [128, 128, 128]
-ADDED_UNITS = [384, 128, 128]
+TOKEN_UNITS = [256, 256, 256, 128, 128]
 
 
 def starts(widths):
@@ -112,9 +110,6 @@ def tile_moe_sup_lin_silu_kernel(
         nc.sync.dma_start(pos_b[:], pos2)
         gates = keep.tile([P, 2, T], F32)
         nc.sync.dma_start(out=gates[:], in_=gate.rearrange("r p t -> p r t"))
-
-        ident = keep.tile([P, P], F32, name="ident", tag="w1w_rest", align_bytes=64)
-        make_identity(nc, ident[:])
 
         h = [keep.tile([P, T], U32, name=f"h{u}", align_bytes=64) for u in range(2)]
 
@@ -255,67 +250,35 @@ def tile_moe_sup_lin_silu_kernel(
             else:
                 nc.vector.tensor_copy(out=y[:, a : a + w], in_=sums[c][:, 0:w])
 
-        first_terms = {}
-        second_terms = {}
+        units = list(zip(starts(TOKEN_UNITS), TOKEN_UNITS))
+        first_terms = [keep.tile([P, w], F32, name=f"first_term{t}") for t, w in units]
+        plain = [keep.tile([P, w], F32, name=f"plain{t}") for t, w in units]
+        second_terms = [keep.tile([P, w], F32, name=f"second_term{t}") for t, w in units]
+        for c, (t, w) in enumerate(units):
+            nc.scalar.activation(plain[c][:], y[:].indirect(pos_b[:, t // 16 : (t + w) // 16]), COPY)
 
-        def fetch(terms, r, t, w):
-            term = keep.tile([P, w], F32, name=f"term{r}_{t}")
+        def fetch_first(c):
+            t, w = units[c]
             nc.vector.tensor_tensor(
-                term[:], y[:].indirect((pos_a, pos_b)[r][:, t // 16 : (t + w) // 16]), gates[:, r, t : t + w], MULT
+                first_terms[c][:], y[:].indirect(pos_a[:, t // 16 : (t + w) // 16]), gates[:, 0, t : t + w], MULT
             )
-            for a in range(0, w, P):
-                terms[t + a] = (term, a)
 
-        def piece(terms, t, w):
-            term, a = terms[t]
-            return term[:, a : a + w]
+        def weigh_second(c):
+            t, w = units[c]
+            nc.vector.tensor_tensor(second_terms[c][:], plain[c][:], gates[:, 1, t : t + w], MULT)
 
-        turned = {}
-
-        def turn_and_add(c, t, w):
-            turned[c] = bank(c % 2)
-            for a in range(0, w, P):
-                for r, terms in enumerate((first_terms, second_terms)):
-                    nc.tensor.matmul(
-                        turned[c][:, a : a + P],
-                        piece(terms, t + a, P),
-                        ident[:],
-                        start=(r == 0),
-                        stop=(r == 1),
-                        is_transpose=True,
-                    )
-
-        def turn_back(c, t, w):
-            by_token = keep.tile([P, w], F32, name=f"by_token{c}")
-            nc.scalar.copy(out=by_token[:], in_=turned[c][:, 0:w])
-            back = bank(4 + c)
-            for a in range(0, w, P):
-                nc.tensor.transpose(back[:, a : a + P], by_token[:, a : a + P], ident[:])
+        def add_and_store(c):
+            t, w = units[c]
             total = keep.tile([P, w], F32, name=f"total{t}")
-            nc.scalar.copy(out=total[:], in_=back[:, 0:w])
-            nc.scalar.dma_start(out=out[:, t : t + w], in_=total[:])
-
-        def add_terms(t, w):
-            total = keep.tile([P, w], F32, name=f"total{t}")
-            nc.vector.tensor_tensor(total[:], piece(first_terms, t, w), piece(second_terms, t, w), ADD)
+            nc.vector.tensor_tensor(total[:], first_terms[c][:], second_terms[c][:], ADD)
             nc.sync.dma_start(out=out[:, t : t + w], in_=total[:])
 
-        turned_tokens = sum(TURNED_UNITS)
-        units = list(zip(starts(TURNED_UNITS), TURNED_UNITS))
-        fetch(first_terms, 0, *units[0])
-        fetch(second_terms, 1, *units[0])
-        fetch(first_terms, 0, units[1][0], turned_tokens - units[1][0])
-        for t, w in units[1:]:
-            fetch(second_terms, 1, t, w)
-        fetch(first_terms, 0, turned_tokens, T - turned_tokens)
-        added = [(turned_tokens + t, w) for t, w in zip(starts(ADDED_UNITS), ADDED_UNITS)]
-        fetch(second_terms, 1, *added[0])
-        for c in range(1, len(added)):
-            fetch(second_terms, 1, *added[c])
-            add_terms(*added[c - 1])
-        add_terms(*added[-1])
-        turn_and_add(0, *units[0])
-        for c in range(len(units)):
-            if c + 1 < len(units):
-                turn_and_add(c + 1, *units[c + 1])
-            turn_back(c, *units[c])
+        last = len(units) - 1
+        fetch_first(0)
+        for c in range(last + 1):
+            if c < last:
+                fetch_first(c + 1)
+            weigh_second(c)
+            if c > 0:
+                add_and_store(c - 1)
+        add_and_store(last)

@@ -21,9 +21,9 @@ ADD = mybir.AluOpType.add
 P = 128
 PASSES = K // 512
 S = E * C
-HALF = T // 2
+WARM_UPS = 5
 SLOT_CHUNKS = [(0, 512), (512, 512), (1024, 256), (1280, 256), (1536, 256), (1792, 128), (1920, 128)]
-UPPER_PIECES = [256, 128, 128]
+TOKEN_GROUPS = [256, 256, 256, 128, 128]
 BACK = 640
 FIRST_GATHERS = [768, 640]
 WOVEN_START = 0
@@ -31,7 +31,8 @@ WOVEN_PIECES = [512, 512]
 SECOND_GATHERS = [384]
 BACK_GATHERS = [384, 256]
 VECTOR_COPIES = (3, 4, 5)
-TOKEN_UNITS = [256, 256, 256, 128, 128]
+BOTH_UNITS = [256, 128]
+SHARED_UNITS = [256, 256, 128]
 
 
 def starts(widths):
@@ -50,7 +51,7 @@ def tile_moe_sup_lin_silu_kernel(
             return psum.tile([P, 512], F32, name=f"bank{b}", tag=f"bank{b}")
 
         w1w_first = keep.tile([P, 1, 2 * H], U8, align_bytes=64)
-        w1w_rest = keep.tile([P, PASSES - 1, 2 * H], U8, tag="w1w_rest", align_bytes=64)
+        w1w_rest = keep.tile([P, PASSES - 1, 2 * H], U8, align_bytes=64)
         w1s_raw = keep.tile([P, PASSES, H], U8, align_bytes=64)
         xs = keep.tile([P, PASSES, T], U8, align_bytes=64)
         w2w = keep.tile([P, E, 2 * N], U8, align_bytes=64)
@@ -60,26 +61,29 @@ def tile_moe_sup_lin_silu_kernel(
         nc.vector.memset(w1s_raw[:].bitcast(I32), 0)
         nc.vector.memset(xs[:].bitcast(I32), 0)
 
-        w1_rows = w1_words.rearrange("s p n -> p s n").bitcast(I32)
-        nc.sync.dma_start(out=w1w_first[:].bitcast(I32), in_=w1_rows[:, 0:1, :])
-
         def load_scale_rows(plane, source, r):
             nc.sync.dma_start(
                 out=plane[r:P:32].bitcast(I32), in_=source[:, r:16:4, :].rearrange("s b n -> b s n").bitcast(I32)
             )
 
+        groups = list(zip(starts(TOKEN_GROUPS), TOKEN_GROUPS))
+        w1_rows = w1_words.rearrange("s p n -> p s n").bitcast(I32)
+        x_first = keep.tile([P, TOKEN_GROUPS[0]], I32, align_bytes=64)
+        x_group = [
+            keep.tile([P, PASSES, w], I32, name=f"x_group{g}", tag=f"x_group{g}", align_bytes=64)
+            for g, w in enumerate(TOKEN_GROUPS)
+        ]
+        nc.sync.dma_start(out=x_first[:], in_=xw[:, 0, 0 : TOKEN_GROUPS[0]])
+        nc.sync.dma_start(out=w1w_first[:].bitcast(I32), in_=w1_rows[:, 0:1, :])
         for r in range(4):
             load_scale_rows(w1s_raw, w1_scales, r)
-        x_lo = [keep.tile([P, HALF], I32, name=f"x_lo{s}", align_bytes=64) for s in range(PASSES)]
-        x_up = keep.tile([P, PASSES, HALF], I32, align_bytes=64)
+        nc.sync.dma_start(out=w1w_rest[:].bitcast(I32), in_=w1_rows[:, 1:PASSES, :])
+        nc.sync.dma_start(out=x_group[0][:, 1:, :], in_=xw[:, 1:, 0 : TOKEN_GROUPS[0]])
         for r in range(4):
             load_scale_rows(xs, x_scales, r)
-        nc.sync.dma_start(out=x_lo[0][:], in_=xw[:, 0, 0:HALF])
-        nc.sync.dma_start(out=w1w_rest[:].bitcast(I32), in_=w1_rows[:, 1:PASSES, :])
-        for s in range(1, PASSES):
-            nc.sync.dma_start(out=x_lo[s][:], in_=xw[:, s, 0:HALF])
-        for a, w in zip(starts(UPPER_PIECES), UPPER_PIECES):
-            nc.sync.dma_start(out=x_up[:, :, a : a + w], in_=xw[:, :, HALF + a : HALF + a + w])
+        for g in range(1, len(groups)):
+            t0, w = groups[g]
+            nc.sync.dma_start(out=x_group[g][:], in_=xw[:, :, t0 : t0 + w])
         slot_list = keep.tile([P, S // 16], U16)
         nc.sync.dma_start(slot_list[:], offs)
 
@@ -116,68 +120,46 @@ def tile_moe_sup_lin_silu_kernel(
         def h_view(u):
             return h[u][:].bitcast(BF16).rearrange("p (t e) -> p t e", e=2)
 
-        def first_layer(acc, u, e, t0, width):
+        def first_layer(b, u, g):
+            t0, w = groups[g]
+            acc = bank(b)
             for s in range(PASSES):
-                if t0 < HALF:
-                    rhs = x_lo[s][:, t0 : t0 + width]
-                else:
-                    rhs = x_up[:, s, t0 - HALF : t0 - HALF + width]
-                nc.tensor.matmul_mx(
-                    out=acc,
-                    lhsT=w1w[u][:, e, s, :].bitcast(FP4X4),
-                    lhsT_scale=w1s[u][:, e, s, :],
-                    rhs=rhs.bitcast(FP8X4),
-                    rhs_scale=xs[:, s, t0 : t0 + width],
-                    start=(s == 0),
-                    stop=(s == PASSES - 1),
-                )
-
-        def wide(b, u, e, t0):
-            acc = bank(b)
-            first_layer(acc[:], u, e, t0, HALF)
-            nc.scalar.activation(h_view(u)[:, t0 : t0 + HALF, e], acc[:], SILU)
-
-        def narrow(b, u, t0, groups):
-            acc = bank(b)
-            for j in range(groups):
+                rhs = x_first[:] if (g == 0 and s == 0) else x_group[g][:, s, :]
                 for e in range(2):
-                    first_layer(acc[:, P * (2 * j + e) : P * (2 * j + e + 1)], u, e, t0 + P * j, P)
+                    nc.tensor.matmul_mx(
+                        out=acc[:, e * w : (e + 1) * w],
+                        lhsT=w1w[u][:, e, s, :].bitcast(FP4X4),
+                        lhsT_scale=w1s[u][:, e, s, :],
+                        rhs=rhs.bitcast(FP8X4),
+                        rhs_scale=xs[:, s, t0 : t0 + w],
+                        start=(s == 0 and e == 0),
+                        stop=(s == PASSES - 1 and e == 1),
+                    )
             nc.scalar.activation(
-                h_view(u)[:, t0 : t0 + P * groups, :].rearrange("p (j t) e -> p j t e", t=P),
-                acc[:, 0 : 2 * P * groups].rearrange("p (j e t) -> p j t e", e=2, t=P),
-                SILU,
+                h_view(u)[:, t0 : t0 + w, :], acc[:, 0 : 2 * w].rearrange("p (e t) -> p t e", e=2), SILU
             )
-            return acc
+
+        warm = bank(7)
+        for j in range(WARM_UPS):
+            nc.tensor.matmul_mx(
+                out=warm[:, 0:256],
+                lhsT=x_first[:, 0:64].bitcast(U8).bitcast(FP4X4),
+                lhsT_scale=w1s_raw[:, 0, 0:P],
+                rhs=x_first[:].bitcast(FP8X4),
+                rhs_scale=w1s_raw[:, 0, 0:256],
+                start=True,
+                stop=True,
+            )
 
         planes = keep.tile([P, 2, T], BF16, tag="planes", align_bytes=64)
-        accs = [bank(e) for e in range(2)]
-        for e in range(2):
-            first_layer(accs[e][:], 0, e, 0, HALF)
-        nc.scalar.activation(planes[:, 0, 0:HALF], accs[0][:], SILU)
-        for a in range(0, HALF, 256):
-            nc.scalar.activation(planes[:, 1, a : a + 256], accs[1][:, a : a + 256], SILU)
-            nc.vector.tensor_copy(
-                out=h_view(0)[:, a : a + 256, :], in_=planes[:, :, a : a + 256].rearrange("p e t -> p t e")
-            )
-
-        def part(t0, w):
-            nc.vector.tensor_copy(
+        for g, (t0, w) in enumerate(groups):
+            first_layer(g, 0, g)
+            engine = nc.gpsimd if g == len(groups) - 1 else nc.vector
+            engine.tensor_copy(
                 out=planes[:, :, t0 : t0 + w], in_=h_view(0)[:, t0 : t0 + w, :].rearrange("p t e -> p e t")
             )
-
-        narrow(2, 0, HALF, 2)
-        part(HALF, 2 * P)
-        narrow(3, 0, HALF + 2 * P, 1)
-        part(HALF + 2 * P, P)
-        narrow(4, 0, HALF + 3 * P, 1)
-        nc.gpsimd.tensor_copy(
-            out=planes[:, :, T - P : T], in_=h_view(0)[:, T - P : T, :].rearrange("p t e -> p e t")
-        )
-        wide(5, 1, 0, HALF)
-        wide(6, 1, 1, HALF)
-        narrow(3, 1, 0, 2)
-        narrow(4, 1, 2 * P, 1)
-        narrow(5, 1, 3 * P, 1)
+        for g in range(len(groups)):
+            first_layer(2 + g % 3, 1, g)
 
         y = keep.tile([P, S], F32)
         codes = keep.tile([P, S], U32, align_bytes=64)
@@ -200,7 +182,7 @@ def tile_moe_sup_lin_silu_kernel(
             else:
                 values = grouped[:, 4 * a : 4 * (a + w)]
             nc.vector.quantize_mx(out=codes[:, a : a + w].bitcast(FP8X4), scales=scales[:, a : a + w], in_=values)
-            acc = bank((0, 1, 2, 7, 5, 6, 3)[c])
+            acc = bank((0, 1, 5, 6, 7, 2, 4)[c])
             step = min(w, C)
             for j in range(0, w, step):
                 e = (a + j) // C
@@ -224,7 +206,7 @@ def tile_moe_sup_lin_silu_kernel(
                 )
 
         rest = keep.tile([P, 2, S - BACK], U32)
-        back = keep.tile([P, 2, BACK], U32, name="back", tag="x_lo2", align_bytes=64)
+        back = keep.tile([P, 2, BACK], U32, name="back", tag="x_group4", align_bytes=64)
         for a, w in zip(starts(FIRST_GATHERS), FIRST_GATHERS):
             gather(rest, 0, 0, a, w)
         gather_rows(back, S - BACK, BACK)
@@ -250,35 +232,39 @@ def tile_moe_sup_lin_silu_kernel(
             else:
                 nc.vector.tensor_copy(out=y[:, a : a + w], in_=sums[c][:, 0:w])
 
-        units = list(zip(starts(TOKEN_UNITS), TOKEN_UNITS))
-        first_terms = [keep.tile([P, w], F32, name=f"first_term{t}") for t, w in units]
+        def fetched(r, t, w):
+            return y[:].indirect((pos_a, pos_b)[r][:, t // 16 : (t + w) // 16])
+
+        def add_and_store(t, w, first, second):
+            total = keep.tile([P, w], F32, name=f"total{t}")
+            nc.vector.tensor_tensor(total[:], first, second, ADD)
+            nc.sync.dma_start(out=out[:, t : t + w], in_=total[:])
+
+        both = sum(BOTH_UNITS)
+        both_units = list(zip(starts(BOTH_UNITS), BOTH_UNITS))
+        units = [(both + t, w) for t, w in zip(starts(SHARED_UNITS), SHARED_UNITS)]
+        both_plain = [keep.tile([P, 2, w], F32, name=f"both_plain{t}") for t, w in both_units]
+        both_terms = keep.tile([P, 2, both], F32)
         plain = [keep.tile([P, w], F32, name=f"plain{t}") for t, w in units]
         second_terms = [keep.tile([P, w], F32, name=f"second_term{t}") for t, w in units]
+        first_terms = keep.tile([P, T - both], F32)
+        for c, (t, w) in enumerate(both_units):
+            for r in range(2):
+                nc.scalar.activation(both_plain[c][:, r, :], fetched(r, t, w), COPY)
         for c, (t, w) in enumerate(units):
-            nc.scalar.activation(plain[c][:], y[:].indirect(pos_b[:, t // 16 : (t + w) // 16]), COPY)
+            nc.scalar.activation(plain[c][:], fetched(1, t, w), COPY)
 
-        def fetch_first(c):
-            t, w = units[c]
-            nc.vector.tensor_tensor(
-                first_terms[c][:], y[:].indirect(pos_a[:, t // 16 : (t + w) // 16]), gates[:, 0, t : t + w], MULT
-            )
+        nc.vector.tensor_tensor(first_terms[:], fetched(0, both, T - both), gates[:, 0, both:T], MULT)
+        for c, (t, w) in enumerate(both_units):
+            nc.vector.tensor_tensor(both_terms[:, :, t : t + w], both_plain[c][:], gates[:, :, t : t + w], MULT)
 
         def weigh_second(c):
             t, w = units[c]
             nc.vector.tensor_tensor(second_terms[c][:], plain[c][:], gates[:, 1, t : t + w], MULT)
 
-        def add_and_store(c):
-            t, w = units[c]
-            total = keep.tile([P, w], F32, name=f"total{t}")
-            nc.vector.tensor_tensor(total[:], first_terms[c][:], second_terms[c][:], ADD)
-            nc.sync.dma_start(out=out[:, t : t + w], in_=total[:])
-
-        last = len(units) - 1
-        fetch_first(0)
-        for c in range(last + 1):
-            if c < last:
-                fetch_first(c + 1)
-            weigh_second(c)
-            if c > 0:
-                add_and_store(c - 1)
-        add_and_store(last)
+        weigh_second(0)
+        add_and_store(0, both, both_terms[:, 0, :], both_terms[:, 1, :])
+        for c, (t, w) in enumerate(units):
+            if c + 1 < len(units):
+                weigh_second(c + 1)
+            add_and_store(t, w, first_terms[:, t - both : t - both + w], second_terms[c][:])

@@ -68,22 +68,31 @@ def tile_moe_sup_lin_silu_kernel(
 
         groups = list(zip(starts(TOKEN_GROUPS), TOKEN_GROUPS))
         w1_rows = w1_words.rearrange("s p n -> p s n").bitcast(I32)
-        x_first = keep.tile([P, TOKEN_GROUPS[0]], I32, align_bytes=64)
-        x_group = [
-            keep.tile([P, PASSES, w], I32, name=f"x_group{g}", tag=f"x_group{g}", align_bytes=64)
-            for g, w in enumerate(TOKEN_GROUPS)
-        ]
-        nc.sync.dma_start(out=x_first[:], in_=xw[:, 0, 0 : TOKEN_GROUPS[0]])
+        x_words_of = {}
+
+        def load_x(g, first, last):
+            t0, w = groups[g]
+            name = f"x_piece{g}_{first}"
+            piece = keep.tile([P, last - first, w], I32, name=name, tag=name, align_bytes=64)
+            nc.sync.dma_start(out=piece[:], in_=xw[:, first:last, t0 : t0 + w])
+            for s in range(first, last):
+                x_words_of[g, s] = piece[:, s - first, :]
+
+        load_x(0, 0, 1)
         nc.sync.dma_start(out=w1w_first[:].bitcast(I32), in_=w1_rows[:, 0:1, :])
         for r in range(4):
             load_scale_rows(w1s_raw, w1_scales, r)
+        load_scale_rows(xs, x_scales, 0)
         nc.sync.dma_start(out=w1w_rest[:].bitcast(I32), in_=w1_rows[:, 1:PASSES, :])
-        nc.sync.dma_start(out=x_group[0][:, 1:, :], in_=xw[:, 1:, 0 : TOKEN_GROUPS[0]])
-        for r in range(4):
+        for r in range(1, 4):
             load_scale_rows(xs, x_scales, r)
+        load_x(0, 1, PASSES)
         for g in range(1, len(groups)):
-            t0, w = groups[g]
-            nc.sync.dma_start(out=x_group[g][:], in_=xw[:, :, t0 : t0 + w])
+            if TOKEN_GROUPS[g] > P:
+                load_x(g, 0, PASSES - 1)
+                load_x(g, PASSES - 1, PASSES)
+            else:
+                load_x(g, 0, PASSES)
         slot_list = keep.tile([P, S // 16], U16)
         nc.sync.dma_start(slot_list[:], offs)
 
@@ -120,21 +129,21 @@ def tile_moe_sup_lin_silu_kernel(
         def h_view(u):
             return h[u][:].bitcast(BF16).rearrange("p (t e) -> p t e", e=2)
 
-        def first_layer(b, u, g):
+        def first_pass(acc, u, g, s):
             t0, w = groups[g]
-            acc = bank(b)
-            for s in range(PASSES):
-                rhs = x_first[:] if (g == 0 and s == 0) else x_group[g][:, s, :]
-                for e in range(2):
-                    nc.tensor.matmul_mx(
-                        out=acc[:, e * w : (e + 1) * w],
-                        lhsT=w1w[u][:, e, s, :].bitcast(FP4X4),
-                        lhsT_scale=w1s[u][:, e, s, :],
-                        rhs=rhs.bitcast(FP8X4),
-                        rhs_scale=xs[:, s, t0 : t0 + w],
-                        start=(s == 0 and e == 0),
-                        stop=(s == PASSES - 1 and e == 1),
-                    )
+            for e in range(2):
+                nc.tensor.matmul_mx(
+                    out=acc[:, e * w : (e + 1) * w],
+                    lhsT=w1w[u][:, e, s, :].bitcast(FP4X4),
+                    lhsT_scale=w1s[u][:, e, s, :],
+                    rhs=x_words_of[g, s].bitcast(FP8X4),
+                    rhs_scale=xs[:, s, t0 : t0 + w],
+                    start=(s == 0 and e == 0),
+                    stop=(s == PASSES - 1 and e == 1),
+                )
+
+        def silu(acc, u, g):
+            t0, w = groups[g]
             nc.scalar.activation(
                 h_view(u)[:, t0 : t0 + w, :], acc[:, 0 : 2 * w].rearrange("p (e t) -> p t e", e=2), SILU
             )
@@ -143,9 +152,9 @@ def tile_moe_sup_lin_silu_kernel(
         for j in range(WARM_UPS):
             nc.tensor.matmul_mx(
                 out=warm[:, 0:256],
-                lhsT=x_first[:, 0:64].bitcast(U8).bitcast(FP4X4),
+                lhsT=x_words_of[0, 0][:, 0:64].bitcast(U8).bitcast(FP4X4),
                 lhsT_scale=w1s_raw[:, 0, 0:P],
-                rhs=x_first[:].bitcast(FP8X4),
+                rhs=x_words_of[0, 0].bitcast(FP8X4),
                 rhs_scale=w1s_raw[:, 0, 0:256],
                 start=True,
                 stop=True,
@@ -153,13 +162,19 @@ def tile_moe_sup_lin_silu_kernel(
 
         planes = keep.tile([P, 2, T], BF16, tag="planes", align_bytes=64)
         for g, (t0, w) in enumerate(groups):
-            first_layer(g, 0, g)
+            acc = bank(g)
+            for s in range(PASSES):
+                first_pass(acc, 0, g, s)
+            silu(acc, 0, g)
             engine = nc.gpsimd if g == len(groups) - 1 else nc.vector
             engine.tensor_copy(
                 out=planes[:, :, t0 : t0 + w], in_=h_view(0)[:, t0 : t0 + w, :].rearrange("p t e -> p e t")
             )
         for g in range(len(groups)):
-            first_layer(2 + g % 3, 1, g)
+            acc = bank(2 + g % 3)
+            for s in range(PASSES):
+                first_pass(acc, 1, g, s)
+            silu(acc, 1, g)
 
         y = keep.tile([P, S], F32)
         codes = keep.tile([P, S], U32, align_bytes=64)
@@ -206,7 +221,7 @@ def tile_moe_sup_lin_silu_kernel(
                 )
 
         rest = keep.tile([P, 2, S - BACK], U32)
-        back = keep.tile([P, 2, BACK], U32, name="back", tag="x_group4", align_bytes=64)
+        back = keep.tile([P, 2, BACK], U32, name="back", tag="x_piece4_0", align_bytes=64)
         for a, w in zip(starts(FIRST_GATHERS), FIRST_GATHERS):
             gather(rest, 0, 0, a, w)
         gather_rows(back, S - BACK, BACK)
@@ -244,27 +259,40 @@ def tile_moe_sup_lin_silu_kernel(
         both_units = list(zip(starts(BOTH_UNITS), BOTH_UNITS))
         units = [(both + t, w) for t, w in zip(starts(SHARED_UNITS), SHARED_UNITS)]
         both_plain = [keep.tile([P, 2, w], F32, name=f"both_plain{t}") for t, w in both_units]
-        both_terms = keep.tile([P, 2, both], F32)
+        both_terms = [keep.tile([P, 2, w], F32, name=f"both_terms{t}") for t, w in both_units]
         plain = [keep.tile([P, w], F32, name=f"plain{t}") for t, w in units]
         second_terms = [keep.tile([P, w], F32, name=f"second_term{t}") for t, w in units]
         first_terms = keep.tile([P, T - both], F32)
-        for c, (t, w) in enumerate(both_units):
-            for r in range(2):
-                nc.scalar.activation(both_plain[c][:, r, :], fetched(r, t, w), COPY)
+
         for c, (t, w) in enumerate(units):
+            if c < len(both_units):
+                for r in range(2):
+                    nc.scalar.activation(both_plain[c][:, r, :], fetched(r, *both_units[c]), COPY)
             nc.scalar.activation(plain[c][:], fetched(1, t, w), COPY)
 
-        nc.vector.tensor_tensor(first_terms[:], fetched(0, both, T - both), gates[:, 0, both:T], MULT)
-        for c, (t, w) in enumerate(both_units):
-            nc.vector.tensor_tensor(both_terms[:, :, t : t + w], both_plain[c][:], gates[:, :, t : t + w], MULT)
+        def weigh_both(c):
+            t, w = both_units[c]
+            nc.vector.tensor_tensor(both_terms[c][:], both_plain[c][:], gates[:, :, t : t + w], MULT)
 
         def weigh_second(c):
             t, w = units[c]
             nc.vector.tensor_tensor(second_terms[c][:], plain[c][:], gates[:, 1, t : t + w], MULT)
 
-        weigh_second(0)
-        add_and_store(0, both, both_terms[:, 0, :], both_terms[:, 1, :])
-        for c, (t, w) in enumerate(units):
-            if c + 1 < len(units):
-                weigh_second(c + 1)
+        def add_both(c):
+            add_and_store(*both_units[c], both_terms[c][:, 0, :], both_terms[c][:, 1, :])
+
+        def add_shared(c):
+            t, w = units[c]
             add_and_store(t, w, first_terms[:, t - both : t - both + w], second_terms[c][:])
+
+        nc.vector.tensor_tensor(first_terms[:], fetched(0, both, T - both), gates[:, 0, both:T], MULT)
+        weigh_both(0)
+        weigh_second(0)
+        add_both(0)
+        add_shared(0)
+        weigh_both(1)
+        weigh_second(1)
+        add_both(1)
+        weigh_second(2)
+        add_shared(1)
+        add_shared(2)

@@ -21,7 +21,7 @@ ADD = mybir.AluOpType.add
 P = 128
 PASSES = K // 512
 S = E * C
-WARM_UPS = 5
+WARM_UPS = [256, 256, 256, 256, 256, 128]
 SLOT_CHUNKS = [(0, 512), (512, 512), (1024, 256), (1280, 256), (1536, 256), (1792, 128), (1920, 128)]
 TOKEN_GROUPS = [256, 256, 256, 128, 128]
 BACK = 640
@@ -58,7 +58,7 @@ def tile_moe_sup_lin_silu_kernel(
         w2s = keep.tile([P, E, N], U8, align_bytes=64)
 
         xw = x_words.rearrange("s p t d -> p s (t d)").bitcast(I32)
-        nc.vector.memset(w1s_raw[:].bitcast(I32), 0)
+        nc.gpsimd.memset(w1s_raw[:].bitcast(I32), 0)
         nc.vector.memset(xs[:].bitcast(I32), 0)
 
         def load_scale_rows(plane, source, r):
@@ -79,9 +79,9 @@ def tile_moe_sup_lin_silu_kernel(
                 x_words_of[g, s] = piece[:, s - first, :]
 
         load_x(0, 0, 1)
-        nc.sync.dma_start(out=w1w_first[:].bitcast(I32), in_=w1_rows[:, 0:1, :])
         for r in range(4):
             load_scale_rows(w1s_raw, w1_scales, r)
+        nc.sync.dma_start(out=w1w_first[:].bitcast(I32), in_=w1_rows[:, 0:1, :])
         load_scale_rows(xs, x_scales, 0)
         nc.sync.dma_start(out=w1w_rest[:].bitcast(I32), in_=w1_rows[:, 1:PASSES, :])
         for r in range(1, 4):
@@ -149,15 +149,15 @@ def tile_moe_sup_lin_silu_kernel(
             )
 
         warm = bank(7)
-        for j in range(WARM_UPS):
+        for j, w in enumerate(WARM_UPS):
             nc.tensor.matmul_mx(
-                out=warm[:, 0:256],
+                out=warm[:, 0:w],
                 lhsT=x_words_of[0, 0][:, 0:64].bitcast(U8).bitcast(FP4X4),
                 lhsT_scale=w1s_raw[:, 0, 0:P],
-                rhs=x_words_of[0, 0].bitcast(FP8X4),
-                rhs_scale=w1s_raw[:, 0, 0:256],
-                start=True,
-                stop=True,
+                rhs=x_words_of[0, 0][:, 0:w].bitcast(FP8X4),
+                rhs_scale=w1s_raw[:, 0, 0:w],
+                start=(j == 0),
+                stop=(j == len(WARM_UPS) - 1),
             )
 
         planes = keep.tile([P, 2, T], BF16, tag="planes", align_bytes=64)

@@ -29,7 +29,9 @@ FIRST_GATHERS = [768, 640]
 WOVEN_START = 0
 WOVEN_PIECES = [512, 512]
 SECOND_GATHERS = [384]
-BACK_GATHERS = [384, 256]
+BACK_GATHERS = [384, 128]
+BACK_INTERLEAVES = [384, 256]
+LAST = 128
 VECTOR_COPIES = (3, 4, 5)
 BOTH_UNITS = [256, 128]
 SHARED_UNITS = [256, 256, 128]
@@ -170,11 +172,16 @@ def tile_moe_sup_lin_silu_kernel(
             engine.tensor_copy(
                 out=planes[:, :, t0 : t0 + w], in_=h_view(0)[:, t0 : t0 + w, :].rearrange("p t e -> p e t")
             )
+        late_planes = keep.tile([P, 2, T], BF16, align_bytes=64)
         for g in range(len(groups)):
             acc = bank(2 + g % 3)
             for s in range(PASSES):
                 first_pass(acc, 1, g, s)
             silu(acc, 1, g)
+            t0, w = groups[g]
+            nc.gpsimd.tensor_copy(
+                out=late_planes[:, :, t0 : t0 + w], in_=h_view(1)[:, t0 : t0 + w, :].rearrange("p t e -> p e t")
+            )
 
         y = keep.tile([P, S], F32)
         codes = keep.tile([P, S], U32, align_bytes=64)
@@ -212,11 +219,11 @@ def tile_moe_sup_lin_silu_kernel(
                 )
             return acc
 
-        def gather_rows(pairs, a, w):
+        def gather_rows(pairs, base, u, a, w):
             for e in range(2):
                 nc.scalar.activation(
-                    pairs[:, 0, :].bitcast(BF16).rearrange("p (n e) -> p n e", e=2)[:, :, e],
-                    planes[:, e, :].indirect(slot_list[:, a // 16 : (a + w) // 16]),
+                    pairs[:, u, a - base : a - base + w].bitcast(BF16).rearrange("p (n e) -> p n e", e=2)[:, :, e],
+                    (planes, late_planes)[u][:, e, :].indirect(slot_list[:, a // 16 : (a + w) // 16]),
                     COPY,
                 )
 
@@ -224,7 +231,8 @@ def tile_moe_sup_lin_silu_kernel(
         back = keep.tile([P, 2, BACK], U32, name="back", tag="x_piece4_0", align_bytes=64)
         for a, w in zip(starts(FIRST_GATHERS), FIRST_GATHERS):
             gather(rest, 0, 0, a, w)
-        gather_rows(back, S - BACK, BACK)
+        gather_rows(back, S - BACK, 0, S - BACK, BACK)
+        gather_rows(back, S - BACK, 1, S - LAST, LAST)
         grouped = keep.tile([P, 4 * S], BF16, name="grouped", tag="planes", align_bytes=64)
         woven = keep.tile([P, 2 * sum(WOVEN_PIECES)], U32, align_bytes=64)
         for a, w in zip(starts(WOVEN_PIECES), WOVEN_PIECES):
@@ -238,6 +246,7 @@ def tile_moe_sup_lin_silu_kernel(
             interleave(rest, 0, sum(WOVEN_PIECES) + a, w)
         for a, w in zip(starts(BACK_GATHERS), BACK_GATHERS):
             gather(back, S - BACK, 1, S - BACK + a, w)
+        for a, w in zip(starts(BACK_INTERLEAVES), BACK_INTERLEAVES):
             interleave(back, S - BACK, S - BACK + a, w)
         chunks = SLOT_CHUNKS
         sums = [second_layer(c, a, w) for c, (a, w) in enumerate(chunks)]
@@ -264,11 +273,18 @@ def tile_moe_sup_lin_silu_kernel(
         second_terms = [keep.tile([P, w], F32, name=f"second_term{t}") for t, w in units]
         first_terms = keep.tile([P, T - both], F32)
 
-        for c, (t, w) in enumerate(units):
-            if c < len(both_units):
-                for r in range(2):
-                    nc.scalar.activation(both_plain[c][:, r, :], fetched(r, *both_units[c]), COPY)
-            nc.scalar.activation(plain[c][:], fetched(1, t, w), COPY)
+        def fetch_both(c):
+            for r in range(2):
+                nc.scalar.activation(both_plain[c][:, r, :], fetched(r, *both_units[c]), COPY)
+
+        def fetch_second(c):
+            nc.scalar.activation(plain[c][:], fetched(1, *units[c]), COPY)
+
+        fetch_both(0)
+        fetch_second(0)
+        fetch_second(1)
+        fetch_both(1)
+        fetch_second(2)
 
         def weigh_both(c):
             t, w = both_units[c]
@@ -289,10 +305,10 @@ def tile_moe_sup_lin_silu_kernel(
         weigh_both(0)
         weigh_second(0)
         add_both(0)
+        weigh_second(1)
         add_shared(0)
         weigh_both(1)
-        weigh_second(1)
-        add_both(1)
-        weigh_second(2)
         add_shared(1)
+        weigh_second(2)
+        add_both(1)
         add_shared(2)

@@ -24,14 +24,14 @@ S = E * C
 WARM_UPS = [256, 256, 256, 256, 256, 128]
 SLOT_CHUNKS = [(0, 512), (512, 512), (1024, 256), (1280, 256), (1536, 256), (1792, 128), (1920, 128)]
 TOKEN_GROUPS = [256, 256, 256, 128, 128]
-BACK = 640
-FIRST_GATHERS = [768, 640]
+BACK = 512
+FIRST_GATHERS = [768, 768]
 WOVEN_START = 0
-WOVEN_PIECES = [512, 512]
-SECOND_GATHERS = [384]
-BACK_GATHERS = [384, 128]
-BACK_INTERLEAVES = [384, 256]
-LAST = 128
+WOVEN_PIECES = [256, 384, 384]
+SECOND_GATHERS = [512]
+BACK_GATHERS = [256]
+BACK_INTERLEAVES = [256, 256]
+LAST = 256
 VECTOR_COPIES = (3, 4, 5)
 BOTH_UNITS = [256, 128]
 SHARED_UNITS = [256, 256, 128]

@@ -33,8 +33,8 @@ BACK_GATHERS = [256]
 BACK_INTERLEAVES = [256, 256]
 LAST = 256
 VECTOR_COPIES = (3, 4, 5)
-BOTH_UNITS = [256, 128]
-SHARED_UNITS = [256, 256, 128]
+BOTH = 192
+SHARED_UNITS = [256, 256, 192, 128]
 
 
 def starts(widths):
@@ -264,51 +264,30 @@ def tile_moe_sup_lin_silu_kernel(
             nc.vector.tensor_tensor(total[:], first, second, ADD)
             nc.sync.dma_start(out=out[:, t : t + w], in_=total[:])
 
-        both = sum(BOTH_UNITS)
-        both_units = list(zip(starts(BOTH_UNITS), BOTH_UNITS))
-        units = [(both + t, w) for t, w in zip(starts(SHARED_UNITS), SHARED_UNITS)]
-        both_plain = [keep.tile([P, 2, w], F32, name=f"both_plain{t}") for t, w in both_units]
-        both_terms = [keep.tile([P, 2, w], F32, name=f"both_terms{t}") for t, w in both_units]
+        units = [(BOTH + t, w) for t, w in zip(starts(SHARED_UNITS), SHARED_UNITS)]
+        both_plain = keep.tile([P, 2, BOTH], F32)
+        both_terms = keep.tile([P, 2, BOTH], F32)
         plain = [keep.tile([P, w], F32, name=f"plain{t}") for t, w in units]
         second_terms = [keep.tile([P, w], F32, name=f"second_term{t}") for t, w in units]
-        first_terms = keep.tile([P, T - both], F32)
-
-        def fetch_both(c):
-            for r in range(2):
-                nc.scalar.activation(both_plain[c][:, r, :], fetched(r, *both_units[c]), COPY)
-
-        def fetch_second(c):
-            nc.scalar.activation(plain[c][:], fetched(1, *units[c]), COPY)
-
-        fetch_both(0)
-        fetch_second(0)
-        fetch_second(1)
-        fetch_both(1)
-        fetch_second(2)
-
-        def weigh_both(c):
-            t, w = both_units[c]
-            nc.vector.tensor_tensor(both_terms[c][:], both_plain[c][:], gates[:, :, t : t + w], MULT)
+        first_terms = keep.tile([P, T - BOTH], F32)
+        for r in range(2):
+            nc.scalar.activation(both_plain[:, r, :], fetched(r, 0, BOTH), COPY)
+        for c, (t, w) in enumerate(units):
+            nc.scalar.activation(plain[c][:], fetched(1, t, w), COPY)
 
         def weigh_second(c):
             t, w = units[c]
             nc.vector.tensor_tensor(second_terms[c][:], plain[c][:], gates[:, 1, t : t + w], MULT)
 
-        def add_both(c):
-            add_and_store(*both_units[c], both_terms[c][:, 0, :], both_terms[c][:, 1, :])
-
         def add_shared(c):
             t, w = units[c]
-            add_and_store(t, w, first_terms[:, t - both : t - both + w], second_terms[c][:])
+            add_and_store(t, w, first_terms[:, t - BOTH : t - BOTH + w], second_terms[c][:])
 
-        nc.vector.tensor_tensor(first_terms[:], fetched(0, both, T - both), gates[:, 0, both:T], MULT)
-        weigh_both(0)
+        nc.vector.tensor_tensor(first_terms[:], fetched(0, BOTH, T - BOTH), gates[:, 0, BOTH:T], MULT)
+        nc.vector.tensor_tensor(both_terms[:], both_plain[:], gates[:, :, 0:BOTH], MULT)
         weigh_second(0)
-        add_both(0)
-        weigh_second(1)
-        add_shared(0)
-        weigh_both(1)
-        add_shared(1)
-        weigh_second(2)
-        add_both(1)
-        add_shared(2)
+        add_and_store(0, BOTH, both_terms[:, 0, :], both_terms[:, 1, :])
+        for c in range(1, len(units)):
+            weigh_second(c)
+            add_shared(c - 1)
+        add_shared(len(units) - 1)

@@ -33,8 +33,8 @@ BACK_GATHERS = [256]
 BACK_INTERLEAVES = [256, 256]
 LAST = 256
 VECTOR_COPIES = (3, 4, 5)
-BOTH = 192
-SHARED_UNITS = [256, 256, 192, 128]
+BOTH = 256
+SHARED_UNITS = [256, 256, 192, 64]
 
 
 def starts(widths):

from contextlib import ExitStack

import concourse.mybir as mybir

K, T, E, C, H, N = 1536, 1024, 8, 256, 512, 128
FLOPS = 2 * K * H * T + 2 * H * N * E * C

F32 = mybir.dt.float32
BF16 = mybir.dt.bfloat16
I32 = mybir.dt.int32
U32 = mybir.dt.uint32
U16 = mybir.dt.uint16
U8 = mybir.dt.uint8
FP8X4 = mybir.dt.float8_e4m3fn_x4
FP4X4 = mybir.dt.float4_e2m1fn_x4
COPY = mybir.ActivationFunctionType.Copy
SILU = mybir.ActivationFunctionType.Silu
MULT = mybir.AluOpType.mult
ADD = mybir.AluOpType.add

P = 128
PASSES = K // 512
S = E * C
WARM_UPS = [256, 256, 256, 256, 256, 128]
SLOT_CHUNKS = [(0, 512), (512, 512), (1024, 256), (1280, 256), (1536, 256), (1792, 128), (1920, 128)]
TOKEN_GROUPS = [256, 256, 256, 128, 128]
BACK = 512
FIRST_GATHERS = [768, 768]
WOVEN_START = 0
WOVEN_PIECES = [256, 384, 384]
SECOND_GATHERS = [512]
BACK_GATHERS = [256]
BACK_INTERLEAVES = [256, 256]
LAST = 256
VECTOR_COPIES = (3, 4, 5)
BOTH = 256
SHARED_UNITS = [256, 256, 192, 64]


def starts(widths):
    return [sum(widths[:i]) for i in range(len(widths))]


def tile_moe_sup_lin_silu_kernel(
    tc, x_words, x_scales, w1_words, w1_scales, w2_words, w2_scales, gate, offs, pos1, pos2, out
):
    nc = tc.nc
    with ExitStack() as ctx:
        keep = ctx.enter_context(tc.tile_pool(name="keep", bufs=1))
        psum = ctx.enter_context(tc.psum_pool(name="psum", bufs=1))

        def bank(b):
            return psum.tile([P, 512], F32, name=f"bank{b}", tag=f"bank{b}")

        w1w_first = keep.tile([P, 1, 2 * H], U8, align_bytes=64)
        w1w_rest = keep.tile([P, PASSES - 1, 2 * H], U8, align_bytes=64)
        w1s_raw = keep.tile([P, PASSES, H], U8, align_bytes=64)
        xs = keep.tile([P, PASSES, T], U8, align_bytes=64)
        w2w = keep.tile([P, E, 2 * N], U8, align_bytes=64)
        w2s = keep.tile([P, E, N], U8, align_bytes=64)

        xw = x_words.rearrange("s p t d -> p s (t d)").bitcast(I32)
        nc.gpsimd.memset(w1s_raw[:].bitcast(I32), 0)
        nc.vector.memset(xs[:].bitcast(I32), 0)

        def load_scale_rows(plane, source, r):
            nc.sync.dma_start(
                out=plane[r:P:32].bitcast(I32), in_=source[:, r:16:4, :].rearrange("s b n -> b s n").bitcast(I32)
            )

        groups = list(zip(starts(TOKEN_GROUPS), TOKEN_GROUPS))
        w1_rows = w1_words.rearrange("s p n -> p s n").bitcast(I32)
        x_words_of = {}

        def load_x(g, first, last):
            t0, w = groups[g]
            name = f"x_piece{g}_{first}"
            piece = keep.tile([P, last - first, w], I32, name=name, tag=name, align_bytes=64)
            nc.sync.dma_start(out=piece[:], in_=xw[:, first:last, t0 : t0 + w])
            for s in range(first, last):
                x_words_of[g, s] = piece[:, s - first, :]

        load_x(0, 0, 1)
        for r in range(4):
            load_scale_rows(w1s_raw, w1_scales, r)
        nc.sync.dma_start(out=w1w_first[:].bitcast(I32), in_=w1_rows[:, 0:1, :])
        load_scale_rows(xs, x_scales, 0)
        nc.sync.dma_start(out=w1w_rest[:].bitcast(I32), in_=w1_rows[:, 1:PASSES, :])
        for r in range(1, 4):
            load_scale_rows(xs, x_scales, r)
        load_x(0, 1, PASSES)
        for g in range(1, len(groups)):
            if TOKEN_GROUPS[g] > P:
                load_x(g, 0, PASSES - 1)
                load_x(g, PASSES - 1, PASSES)
            else:
                load_x(g, 0, PASSES)
        slot_list = keep.tile([P, S // 16], U16)
        nc.sync.dma_start(slot_list[:], offs)

        w1w = [keep.tile([P, 2, PASSES, 2 * P], U8, name=f"w1w{u}", align_bytes=64) for u in range(2)]
        w1s = [keep.tile([P, 2, PASSES, P], U8, name=f"w1s{u}", align_bytes=64) for u in range(2)]

        def regroup_words(u, raw, first, count):
            nc.vector.tensor_copy(
                out=w1w[u][:, :, first : first + count, :].bitcast(U16),
                in_=raw[:].bitcast(U16).rearrange("p s (m t) -> p t s m", t=4)[:, 2 * u : 2 * u + 2],
            )

        for u in range(2):
            regroup_words(u, w1w_first, 0, 1)
            nc.vector.tensor_copy(
                out=w1s[u][:],
                in_=w1s_raw[:].rearrange("p s (m t) -> p t s m", t=4)[:, 2 * u : 2 * u + 2],
            )
            regroup_words(u, w1w_rest, 1, PASSES - 1)

        nc.vector.memset(w2s[:].bitcast(I32), 0)
        nc.sync.dma_start(out=w2w[:].bitcast(I32), in_=w2_words.rearrange("e g p n -> p (e g) n").bitcast(I32))
        for r in range(4):
            load_scale_rows(w2s, w2_scales.rearrange("e g b n -> (e g) b n"), r)
        pos_a = keep.tile([P, T // 16], U16)
        pos_b = keep.tile([P, T // 16], U16)
        nc.sync.dma_start(pos_a[:], pos1)
        nc.sync.dma_start(pos_b[:], pos2)
        gates = keep.tile([P, 2, T], F32)
        nc.sync.dma_start(out=gates[:], in_=gate.rearrange("r p t -> p r t"))

        h = [keep.tile([P, T], U32, name=f"h{u}", align_bytes=64) for u in range(2)]

        def h_view(u):
            return h[u][:].bitcast(BF16).rearrange("p (t e) -> p t e", e=2)

        def first_pass(acc, u, g, s):
            t0, w = groups[g]
            for e in range(2):
                nc.tensor.matmul_mx(
                    out=acc[:, e * w : (e + 1) * w],
                    lhsT=w1w[u][:, e, s, :].bitcast(FP4X4),
                    lhsT_scale=w1s[u][:, e, s, :],
                    rhs=x_words_of[g, s].bitcast(FP8X4),
                    rhs_scale=xs[:, s, t0 : t0 + w],
                    start=(s == 0 and e == 0),
                    stop=(s == PASSES - 1 and e == 1),
                )

        def silu(acc, u, g):
            t0, w = groups[g]
            nc.scalar.activation(
                h_view(u)[:, t0 : t0 + w, :], acc[:, 0 : 2 * w].rearrange("p (e t) -> p t e", e=2), SILU
            )

        warm = bank(7)
        for j, w in enumerate(WARM_UPS):
            nc.tensor.matmul_mx(
                out=warm[:, 0:w],
                lhsT=x_words_of[0, 0][:, 0:64].bitcast(U8).bitcast(FP4X4),
                lhsT_scale=w1s_raw[:, 0, 0:P],
                rhs=x_words_of[0, 0][:, 0:w].bitcast(FP8X4),
                rhs_scale=w1s_raw[:, 0, 0:w],
                start=(j == 0),
                stop=(j == len(WARM_UPS) - 1),
            )

        planes = keep.tile([P, 2, T], BF16, tag="planes", align_bytes=64)
        for g, (t0, w) in enumerate(groups):
            acc = bank(g)
            for s in range(PASSES):
                first_pass(acc, 0, g, s)
            silu(acc, 0, g)
            engine = nc.gpsimd if g == len(groups) - 1 else nc.vector
            engine.tensor_copy(
                out=planes[:, :, t0 : t0 + w], in_=h_view(0)[:, t0 : t0 + w, :].rearrange("p t e -> p e t")
            )
        late_planes = keep.tile([P, 2, T], BF16, align_bytes=64)
        for g in range(len(groups)):
            acc = bank(2 + g % 3)
            for s in range(PASSES):
                first_pass(acc, 1, g, s)
            silu(acc, 1, g)
            t0, w = groups[g]
            nc.gpsimd.tensor_copy(
                out=late_planes[:, :, t0 : t0 + w], in_=h_view(1)[:, t0 : t0 + w, :].rearrange("p t e -> p e t")
            )

        y = keep.tile([P, S], F32)
        codes = keep.tile([P, S], U32, align_bytes=64)
        scales = keep.tile([P, S], U8, align_bytes=64)

        def gather(pairs, base, u, a, w):
            nc.vector.tensor_copy(
                pairs[:, u, a - base : a - base + w], h[u][:].indirect(slot_list[:, a // 16 : (a + w) // 16])
            )

        def interleave(pairs, base, a, w):
            nc.scalar.copy(
                out=grouped[:, 4 * a : 4 * (a + w)].bitcast(F32).rearrange("p (n u) -> p n u", u=2),
                in_=pairs[:, :, a - base : a - base + w].bitcast(F32).rearrange("p u n -> p n u"),
            )

        def second_layer(c, a, w):
            if a < sum(WOVEN_PIECES):
                values = woven[:, 2 * (a - WOVEN_START) : 2 * (a - WOVEN_START + w)].bitcast(BF16)
            else:
                values = grouped[:, 4 * a : 4 * (a + w)]
            nc.vector.quantize_mx(out=codes[:, a : a + w].bitcast(FP8X4), scales=scales[:, a : a + w], in_=values)
            acc = bank((0, 1, 5, 6, 7, 2, 4)[c])
            step = min(w, C)
            for j in range(0, w, step):
                e = (a + j) // C
                nc.tensor.matmul_mx(
                    out=acc[:, j : j + step],
                    lhsT=w2w[:, e, :].bitcast(FP4X4),
                    lhsT_scale=w2s[:, e, :],
                    rhs=codes[:, a + j : a + j + step].bitcast(FP8X4),
                    rhs_scale=scales[:, a + j : a + j + step],
                    start=True,
                    stop=True,
                )
            return acc

        def gather_rows(pairs, base, u, a, w):
            for e in range(2):
                nc.scalar.activation(
                    pairs[:, u, a - base : a - base + w].bitcast(BF16).rearrange("p (n e) -> p n e", e=2)[:, :, e],
                    (planes, late_planes)[u][:, e, :].indirect(slot_list[:, a // 16 : (a + w) // 16]),
                    COPY,
                )

        rest = keep.tile([P, 2, S - BACK], U32)
        back = keep.tile([P, 2, BACK], U32, name="back", tag="x_piece4_0", align_bytes=64)
        for a, w in zip(starts(FIRST_GATHERS), FIRST_GATHERS):
            gather(rest, 0, 0, a, w)
        gather_rows(back, S - BACK, 0, S - BACK, BACK)
        gather_rows(back, S - BACK, 1, S - LAST, LAST)
        grouped = keep.tile([P, 4 * S], BF16, name="grouped", tag="planes", align_bytes=64)
        woven = keep.tile([P, 2 * sum(WOVEN_PIECES)], U32, align_bytes=64)
        for a, w in zip(starts(WOVEN_PIECES), WOVEN_PIECES):
            gather(rest, 0, 1, WOVEN_START + a, w)
            nc.gpsimd.tensor_copy(
                out=woven[:, 2 * a : 2 * (a + w)].rearrange("p (n u) -> p n u", u=2),
                in_=rest[:, :, WOVEN_START + a : WOVEN_START + a + w].rearrange("p u n -> p n u"),
            )
        for a, w in zip(starts(SECOND_GATHERS), SECOND_GATHERS):
            gather(rest, 0, 1, sum(WOVEN_PIECES) + a, w)
            interleave(rest, 0, sum(WOVEN_PIECES) + a, w)
        for a, w in zip(starts(BACK_GATHERS), BACK_GATHERS):
            gather(back, S - BACK, 1, S - BACK + a, w)
        for a, w in zip(starts(BACK_INTERLEAVES), BACK_INTERLEAVES):
            interleave(back, S - BACK, S - BACK + a, w)
        chunks = SLOT_CHUNKS
        sums = [second_layer(c, a, w) for c, (a, w) in enumerate(chunks)]
        for c, (a, w) in enumerate(chunks):
            if c not in VECTOR_COPIES:
                nc.scalar.copy(out=y[:, a : a + w], in_=sums[c][:, 0:w])
            else:
                nc.vector.tensor_copy(out=y[:, a : a + w], in_=sums[c][:, 0:w])

        def fetched(r, t, w):
            return y[:].indirect((pos_a, pos_b)[r][:, t // 16 : (t + w) // 16])

        def add_and_store(t, w, first, second):
            total = keep.tile([P, w], F32, name=f"total{t}")
            nc.vector.tensor_tensor(total[:], first, second, ADD)
            nc.sync.dma_start(out=out[:, t : t + w], in_=total[:])

        units = [(BOTH + t, w) for t, w in zip(starts(SHARED_UNITS), SHARED_UNITS)]
        both_plain = keep.tile([P, 2, BOTH], F32)
        both_terms = keep.tile([P, 2, BOTH], F32)
        plain = [keep.tile([P, w], F32, name=f"plain{t}") for t, w in units]
        second_terms = [keep.tile([P, w], F32, name=f"second_term{t}") for t, w in units]
        first_terms = keep.tile([P, T - BOTH], F32)
        for r in range(2):
            nc.scalar.activation(both_plain[:, r, :], fetched(r, 0, BOTH), COPY)
        for c, (t, w) in enumerate(units):
            nc.scalar.activation(plain[c][:], fetched(1, t, w), COPY)

        def weigh_second(c):
            t, w = units[c]
            nc.vector.tensor_tensor(second_terms[c][:], plain[c][:], gates[:, 1, t : t + w], MULT)

        def add_shared(c):
            t, w = units[c]
            add_and_store(t, w, first_terms[:, t - BOTH : t - BOTH + w], second_terms[c][:])

        nc.vector.tensor_tensor(first_terms[:], fetched(0, BOTH, T - BOTH), gates[:, 0, BOTH:T], MULT)
        nc.vector.tensor_tensor(both_terms[:], both_plain[:], gates[:, :, 0:BOTH], MULT)
        weigh_second(0)
        add_and_store(0, BOTH, both_terms[:, 0, :], both_terms[:, 1, :])
        for c in range(1, len(units)):
            weigh_second(c)
            add_shared(c - 1)
        add_shared(len(units) - 1)
